import numpy as np
import ml_dtypes


def mxq(x, axis, fmt="e4m3"):
    dtype, down = {"e4m3": (ml_dtypes.float8_e4m3fn, 7), "e5m2": (ml_dtypes.float8_e5m2, 14)}[fmt]
    v = np.moveaxis(np.asarray(x, np.float32).astype(ml_dtypes.bfloat16).astype(np.float64), axis, -1)
    blocks = v.reshape(v.shape[:-1] + (-1, 32))
    amax = np.abs(blocks).max(-1, keepdims=True)
    byte = np.maximum(np.where(amax > 0, np.frexp(amax)[1] - 1 + 127, 0) - down, 1)
    scale = np.exp2(byte - 127.0)
    codes = (blocks / scale).astype(np.float32).astype(dtype).astype(np.float64)
    return np.moveaxis((codes * scale).reshape(v.shape), -1, axis)


WIDE = False


def mx_kscale(k):
    if not WIDE:
        return np.ones(k)
    levels = np.array([10, -10, 5, -5, 0])
    if k % 512:
        return np.exp2(np.random.permutation(np.resize(levels, k // 32))).repeat(32)
    a = np.empty((k // 512, 16))
    for p in range(k // 512):
        a[p, :8] = np.random.permutation(np.resize(levels, 8))
        for g in range(8):
            far = levels[np.abs(levels - a[p, g]) >= 10]
            a[p, g + 8] = far[np.random.randint(len(far))]
    return np.exp2(a.ravel()).repeat(32)


def f64(x):
    return np.asarray(x).astype(np.float64)


def striped(idx):
    return np.tile(idx.reshape(-1, 16).T, (8, 1)).astype(np.uint16)


def unstriped(offs):
    return offs[:16].T.reshape(-1).astype(np.int64)


E2M1 = np.array([0.0, 0.5, 1.0, 1.5, 2.0, 3.0, 4.0, 6.0, -0.0, -0.5, -1.0, -1.5, -2.0, -3.0, -4.0, -6.0])


def pack_weight(w, fmt):
    k, n = w.shape
    w = f64(np.asarray(w, np.float32).astype(ml_dtypes.bfloat16)).reshape(k // 32, 32, n)
    amax = np.abs(w).max(1)
    if fmt == "e4m3":
        byte = np.frexp(amax)[1] - 1 + 127 - 7
    else:
        mant, ex = np.frexp(amax / 6.0)
        byte = np.where(mant > 0.5, ex, ex - 1) + 127
    byte = np.clip(np.where(amax > 0, byte, 1), 1, 254)
    scaled = (w * np.exp2(127.0 - byte)[:, None, :]).reshape(k, n).astype(np.float32)
    by_word = np.ascontiguousarray(scaled.reshape(k // 512, 128, 4, n).transpose(0, 1, 3, 2))
    if fmt == "e4m3":
        words = by_word.astype(ml_dtypes.float8_e4m3fn).view(np.uint8)
    else:
        c = by_word.astype(ml_dtypes.float4_e2m1fn).view(np.uint8) & 0xF
        words = (c[..., 0::2] | (c[..., 1::2] << 4)).reshape(k // 512, 128, 2 * n)
    return np.ascontiguousarray(words), np.ascontiguousarray(byte.astype(np.uint8).reshape(k // 512, 16, n))


def unpack_weight(words, scales, fmt):
    g, _, n = scales.shape
    words = np.ascontiguousarray(words).reshape(g, 128, n, -1)
    if fmt == "e4m3":
        vals = words.view(ml_dtypes.float8_e4m3fn).astype(np.float64)
    else:
        nib = np.empty((g, 128, n, 4), np.uint8)
        nib[..., 0::2] = words & 0xF
        nib[..., 1::2] = words >> 4
        vals = E2M1[nib]
    vals = vals * np.repeat(np.exp2(scales.astype(np.float64) - 127.0), 8, axis=1)[..., None]
    return vals.transpose(0, 1, 3, 2).reshape(g * 512, n)


def gelu(v):
    return 0.5 * v * (1.0 + np.tanh(np.sqrt(2.0 / np.pi) * (v + 0.044715 * v**3)))


K, T, E, C, H, TOP, COPIES = 512, 640, 10, 128, 512, 3, 160
PAD = 64


def by_expert(wq, xq):
    return np.concatenate([wq[e].T @ xq[:, e * C:(e + 1) * C] for e in range(E)], axis=1)


def setup_inputs():
    n = np.random.standard_normal
    s = mx_kscale(K)
    u = mx_kscale(H)
    left = TOP * T - E * C - COPIES
    deal = np.repeat(np.arange(E + 2), [C] * E + [COPIES, left]).reshape(TOP, T)[:, np.random.permutation(T)]
    deal = np.take_along_axis(deal, np.argsort(np.random.rand(TOP, T), axis=0), axis=0)
    for _ in range(8):
        s_, t_ = np.random.permutation(T).reshape(2, -1); r = np.random.randint(TOP, size=T // 2); x, y = deal[r, s_].copy(), deal[r, t_].copy()
        ok = ~((deal[:, s_] == y).any(0) | (deal[:, t_] == x).any(0)); deal[r[ok], s_[ok]] = y[ok]; deal[r[ok], t_[ok]] = x[ok]
    order = np.lexsort((np.random.rand(TOP * T), deal.reshape(-1)))[:E * C]
    slot_token = order % T
    pos = np.where(deal == E, E * C + np.arange(T), E * C + T + np.arange(T) % PAD).reshape(-1); pos[order] = np.arange(E * C); pos = pos.reshape(TOP, T)
    g = np.random.uniform(0.5, 1.5, (TOP, T)); g = g / g.sum(0)
    xf = n((K, T))
    x = pack_weight(xf * s[:, None], "e4m3")
    w1 = [pack_weight(m, "e4m3") for m in n((E, K, H)) / np.sqrt(K) / s[None, :, None] * u]
    w2 = [pack_weight(m, "e4m3") for m in n((E, H, K)) / np.sqrt(H) / u[None, :, None]]
    return {
        "x_words": x[0],
        "x_scales": x[1],
        "xr": (xf).astype(np.float32),
        "w1_words": np.stack([m[0] for m in w1]),
        "w1_scales": np.stack([m[1] for m in w1]),
        "w2_words": np.stack([m[0] for m in w2]),
        "w2_scales": np.stack([m[1] for m in w2]),
        "gate": np.stack([np.tile(r, (128, 1)) for r in g]).astype(np.float32),
        "offs": striped(slot_token),
        "pos1": striped(pos[0]),
        "pos2": striped(pos[1]),
        "pos3": striped(pos[2]),
    }


def reference(x_words, x_scales, xr, w1_words, w1_scales, w2_words, w2_scales, gate, offs, pos1, pos2, pos3):
    w1 = np.stack([unpack_weight(w1_words[e], w1_scales[e], "e4m3") for e in range(E)])
    w2 = np.stack([unpack_weight(w2_words[e], w2_scales[e], "e4m3") for e in range(E)])
    idx = unstriped(offs)
    xq = unpack_weight(x_words, x_scales, "e4m3")[:, idx]
    h = gelu(by_expert(w1, xq))
    y = by_expert(w2, mxq(h, 0, "e4m3"))
    y = np.concatenate([y, f64(xr), np.zeros((K, PAD))], axis=1)
    out = sum(f64(gate[r, :1]) * y[:, unstriped(p)] for r, p in enumerate((pos1, pos2, pos3)))
    return out

@@ -1,0 +1,224 @@
+from contextlib import ExitStack
+
+import concourse.mybir as mybir
+from concourse.masks import make_identity
+
+K, T, E, C, H = 512, 640, 10, 128, 512
+SLOTS = E * C
+PAD = 64
+WIDE = SLOTS + T + PAD
+FLOPS = 2 * SLOTS * (K * H + H * K)
+
+F32 = mybir.dt.float32
+BF16 = mybir.dt.bfloat16
+I32 = mybir.dt.int32
+U32 = mybir.dt.uint32
+U16 = mybir.dt.uint16
+U8 = mybir.dt.uint8
+FP8X4 = mybir.dt.float8_e4m3fn_x4
+GELU = mybir.ActivationFunctionType.Gelu_apprx_tanh
+MULT = mybir.AluOpType.mult
+ADD = mybir.AluOpType.add
+
+P = 128
+PAIRS = E // 2
+BLOCKS = K // P
+W2_ROW = 4
+GROUPS = ((0, 4), (4, 8), (8, 10))
+SHARED = ((6, 7, 5), (6, 3, 4))
+W1_LOADS = ((0, 2), (2, 5), (5, 8), (8, 10))
+HALVES = ((0, 3), (3, 5))
+
+
+def tile_moe_cpy_mlp_gelu_kernel(
+    tc, x_words, x_scales, xr, w1_words, w1_scales, w2_words, w2_scales, gate, offs, pos1, pos2, pos3, out
+):
+    nc = tc.nc
+    with ExitStack() as ctx:
+        lists = ctx.enter_context(tc.tile_pool(name="lists", bufs=1))
+        held = ctx.enter_context(tc.tile_pool(name="held", bufs=1))
+        ring = ctx.enter_context(tc.tile_pool(name="ring", bufs=2))
+        psum = ctx.enter_context(tc.psum_pool(name="psum", bufs=1))
+
+        slot_list = lists.tile([P, SLOTS // 16], U16, name="slot_list")
+        choice_lists = [lists.tile([P, T // 16], U16, name="choice_list%d" % r) for r in range(3)]
+
+        xw = held.tile([P, T], U32, name="xw", align_bytes=64)
+        xs = held.tile([P, T], U8, name="xs", align_bytes=64)
+        w1 = held.tile([P, E, H], U32, name="w1", align_bytes=64)
+        w1s = held.tile([P, E, H], U8, name="w1s", align_bytes=64)
+        w2s = held.tile([P, E, K], U8, name="w2s", align_bytes=64)
+        w2a = held.tile([P, E, P], U32, name="w2a", align_bytes=64)
+        w2b = held.tile([P, E, P], U32, name="w2b", align_bytes=64)
+        w2c = held.tile([P, E, 2 * P], U32, name="w2c", align_bytes=64)
+        ys = [held.tile([P, WIDE], F32, name="y%d" % b, align_bytes=64) for b in range(BLOCKS)]
+        gate1 = held.tile([P, T], F32, name="gate1", align_bytes=64)
+        gate23 = held.tile([P, 2, T], F32, name="gate23", align_bytes=64)
+        gates = [gate1[:], gate23[:, 0, :], gate23[:, 1, :]]
+        ident = held.tile([P, P], F32, name="ident", align_bytes=64)
+        hq = [held.tile([P, 2 * C], U32, name="hq%d" % g, align_bytes=64) for g in range(PAIRS)]
+        hs = [held.tile([P, 2 * C], U8, name="hs%d" % g, align_bytes=64) for g in range(PAIRS)]
+
+        def load_words(tile, words):
+            nc.sync.dma_start(tile.bitcast(I32), words.rearrange("e p n d -> p e (n d)").bitcast(I32))
+
+        def load_scales(queue, plane, row, scales, q):
+            queue.dma_start(
+                plane[32 * q + row : 32 * q + row + 4].bitcast(I32),
+                scales[:, 0, 4 * q : 4 * q + 4, :].rearrange("e r n -> r e n").bitcast(I32),
+            )
+
+        def load_xr(b):
+            nc.sync.dma_start(ys[b][:, SLOTS : SLOTS + T], xr[b * P : (b + 1) * P, :])
+
+        nc.vector.memset(xs[:].bitcast(I32), 0)
+        for b in range(BLOCKS):
+            nc.vector.memset(ys[b][:, SLOTS + T :], 0.0)
+
+        make_identity(nc, ident[:])
+
+        nc.sync.dma_start(slot_list[:], offs)
+        for q in range(4):
+            queue = nc.sync if q < 2 else nc.scalar
+            queue.dma_start(xs[32 * q : 32 * q + 4, :].bitcast(I32), x_scales[0, 4 * q : 4 * q + 4, :].bitcast(I32))
+        nc.sync.dma_start(xw[:].bitcast(I32), x_words[0].rearrange("p t d -> p (t d)").bitcast(I32))
+        for i, (lo, hi) in enumerate(W1_LOADS):
+            load_words(w1[:, lo:hi, :], w1_words[lo:hi, 0])
+            if i == 0:
+                for q in range(4):
+                    load_scales(nc.sync, w1s, 0, w1_scales, q)
+        for q in range(4):
+            load_scales(nc.sync, w2s, W2_ROW, w2_scales, q)
+        load_words(w2a[:], w2_words[:, 0, :, 0:P, :])
+        load_xr(0)
+        nc.sync.dma_start(choice_lists[0][:], pos1)
+        nc.sync.dma_start(gate1[:], gate[0])
+        nc.sync.dma_start(choice_lists[1][:], pos2)
+        nc.sync.dma_start(choice_lists[2][:], pos3)
+        nc.sync.dma_start(gate23[:], gate[1:3].rearrange("r p t -> p r t"))
+        load_words(w2b[:], w2_words[:, 0, :, P : 2 * P, :])
+        load_xr(1)
+        load_words(w2c[:], w2_words[:, 0, :, 2 * P :, :])
+        load_xr(2)
+        load_xr(3)
+
+        def w2_codes(e, b):
+            if b == 0:
+                return w2a[:, e, :]
+            if b == 1:
+                return w2b[:, e, :]
+            return w2c[:, e, (b - 2) * P : (b - 1) * P]
+
+        xg = [held.tile([P, 2 * C], U32, name="xg%d" % g, align_bytes=64) for g in range(PAIRS)]
+        xgs = [held.tile([P, 2 * C], U8, name="xgs%d" % g, align_bytes=64) for g in range(PAIRS)]
+        for g in range(PAIRS):
+            picks = slot_list[:, g * 2 * C // 16 : (g + 1) * 2 * C // 16]
+            nc.vector.tensor_copy(xg[g][:], xw[:].indirect(picks))
+            nc.vector.tensor_copy(xgs[g][:], xs[:].indirect(picks))
+
+        def first_layer(g):
+            turned = psum.tile([P, 2, 2, C], F32, name="turned", tag="bank%d" % (3 + g % 3))
+            for a in range(2):
+                e = 2 * g + a
+                pre = psum.tile([P, H], F32, name="pre", tag="bank%d" % (e % 3))
+                nc.tensor.matmul_mx(
+                    out=pre[:],
+                    lhsT=xg[g][:, a * C : (a + 1) * C].bitcast(FP8X4),
+                    lhsT_scale=xgs[g][:, a * C : (a + 1) * C],
+                    rhs=w1[:, e, :].bitcast(FP8X4),
+                    rhs_scale=w1s[:, e, :],
+                    start=True,
+                    stop=True,
+                )
+                h_rows = ring.tile([P, H], BF16, name="h_rows", tag="h_rows", bufs=4, align_bytes=64)
+                nc.scalar.activation(
+                    h_rows[:].rearrange("s (u p d) -> s u p d", u=2, d=2),
+                    pre[:].rearrange("s (p u d) -> s u p d", u=2, d=2),
+                    GELU,
+                )
+                pairs = h_rows[:].bitcast(F32)
+                for u in range(2):
+                    nc.tensor.transpose(turned[:, a, u, :], pairs[:, u * P : (u + 1) * P], ident[:])
+            h_cols = ring.tile([P, 2 * C * 4], BF16, name="h_cols", tag="h_cols", bufs=5, align_bytes=64)
+            dst = h_cols[:].bitcast(F32).rearrange("p (a s u) -> p a s u", a=2, u=2)
+            src = turned[:].rearrange("p a u s -> p a s u")
+            if g < 2:
+                nc.scalar.copy(dst, src)
+            else:
+                nc.vector.tensor_copy(dst, src)
+            nc.vector.quantize_mx(out=hq[g][:].bitcast(FP8X4), scales=hs[g][:], in_=h_cols[:])
+
+        def second_layer(b, i):
+            lo, hi = GROUPS[i]
+            acc = psum.tile([P, 4 * C], F32, name="acc", tag="bank%d" % SHARED[b % 2][i])
+            for e in range(lo, hi):
+                cols = slice((e % 2) * C, (e % 2 + 1) * C)
+                nc.tensor.matmul_mx(
+                    out=acc[:, (e - lo) * C : (e - lo + 1) * C],
+                    lhsT=w2_codes(e, b).bitcast(FP8X4),
+                    lhsT_scale=w2s[W2_ROW:, e, b * P : (b + 1) * P],
+                    rhs=hq[e // 2][:, cols].bitcast(FP8X4),
+                    rhs_scale=hs[e // 2][:, cols],
+                    start=True,
+                    stop=True,
+                )
+            nc.scalar.copy(ys[b][:, lo * C : hi * C], acc[:, : (hi - lo) * C])
+
+        def weighted(b, r, t0, t1, tag, bufs):
+            term = ring.tile([P, t1 - t0], F32, name="term", tag=tag, bufs=bufs, align_bytes=64)
+            nc.vector.tensor_tensor(
+                term[:], ys[b][:].indirect(choice_lists[r][:, t0 // 16 : t1 // 16]), gates[r][:, t0:t1], MULT
+            )
+            return term
+
+        def summed_on_tensor(b, terms):
+            result = ring.tile([P, T], F32, name="result", tag="result", bufs=2, align_bytes=64)
+            for i, (lo, hi) in enumerate(HALVES):
+                n = hi - lo
+                total = psum.tile([P, 3 * P], F32, name="total", tag="bank%d" % SHARED[(b + 1) % 2][i + 1])
+                for j in range(lo, hi):
+                    for r in range(3):
+                        nc.tensor.matmul(
+                            total[:, (j - lo) * P : (j - lo + 1) * P],
+                            lhsT=terms[r][:, j * P : (j + 1) * P],
+                            rhs=ident[:],
+                            is_transpose=True,
+                            start=(r == 0),
+                            stop=(r == 2),
+                        )
+                by_token = ring.tile([P, 3 * P], F32, name="by_token", tag="by_token", bufs=2, align_bytes=64)
+                nc.scalar.copy(by_token[:, : n * P], total[:, : n * P])
+                back = psum.tile([P, 3 * P], F32, name="back", tag="bank%d" % i)
+                for j in range(n):
+                    nc.tensor.transpose(back[:, j * P : (j + 1) * P], by_token[:, j * P : (j + 1) * P], ident[:])
+                nc.scalar.copy(result[:, lo * P : hi * P], back[:, : n * P])
+            nc.sync.dma_start(out[b * P : (b + 1) * P, :], result[:])
+
+        for g in range(PAIRS):
+            first_layer(g)
+        for i in range(len(GROUPS)):
+            second_layer(0, i)
+        for b in range(BLOCKS - 1):
+            for i in range(len(GROUPS)):
+                second_layer(b + 1, i)
+            terms = [weighted(b, r, 0, T, "term", 6) for r in range(3)]
+            summed_on_tensor(b, terms)
+
+        b = BLOCKS - 1
+        half = T // 2
+        a0 = weighted(b, 0, 0, half, "last", 10)
+        b0 = weighted(b, 1, 0, half, "last", 10)
+        a1 = weighted(b, 0, half, T, "last", 10)
+        ab0 = ring.tile([P, half], F32, name="ab0", tag="last", bufs=10, align_bytes=64)
+        nc.vector.tensor_tensor(ab0[:], a0[:], b0[:], ADD)
+        c0 = weighted(b, 2, 0, half, "last", 10)
+        b1 = weighted(b, 1, half, T, "last", 10)
+        abc0 = ring.tile([P, half], F32, name="abc0", tag="last", bufs=10, align_bytes=64)
+        nc.vector.tensor_tensor(abc0[:], ab0[:], c0[:], ADD)
+        nc.sync.dma_start(out[b * P : (b + 1) * P, :half], abc0[:])
+        ab1 = ring.tile([P, half], F32, name="ab1", tag="last", bufs=10, align_bytes=64)
+        nc.vector.tensor_tensor(ab1[:], a1[:], b1[:], ADD)
+        c1 = weighted(b, 2, half, T, "last", 10)
+        abc1 = ring.tile([P, half], F32, name="abc1", tag="last", bufs=10, align_bytes=64)
+        nc.vector.tensor_tensor(abc1[:], ab1[:], c1[:], ADD)
+        nc.sync.dma_start(out[b * P : (b + 1) * P, half:], abc1[:])

@@ -26,7 +26,8 @@ BLOCKS = K // P
 W2_ROW = 4
 GROUPS = ((0, 4), (4, 8), (8, 10))
 SHARED = ((6, 7, 5), (6, 3, 4))
-W1_LOADS = ((0, 2), (2, 5), (5, 8), (8, 10))
+W1_LOADS = ((0, 2), (2, 4), (4, 6), (6, 8), (8, 10))
+PRE_BANKS = ((0, 1), (2, 7))
 HALVES = ((0, 3), (3, 5))
 
 
@@ -52,9 +53,9 @@ def tile_moe_cpy_mlp_gelu_kernel(
         w2b = held.tile([P, E, P], U32, name="w2b", align_bytes=64)
         w2c = held.tile([P, E, 2 * P], U32, name="w2c", align_bytes=64)
         ys = [held.tile([P, WIDE], F32, name="y%d" % b, align_bytes=64) for b in range(BLOCKS)]
-        gate1 = held.tile([P, T], F32, name="gate1", align_bytes=64)
-        gate23 = held.tile([P, 2, T], F32, name="gate23", align_bytes=64)
-        gates = [gate1[:], gate23[:, 0, :], gate23[:, 1, :]]
+        gate_rows = held.tile([P, T], F32, name="gate_rows", align_bytes=64)
+        gate_cols = held.tile([P, T // P, 4], F32, name="gate_cols", align_bytes=64)
+        gates = [held.tile([P, T], F32, name="gate%d" % r, align_bytes=64) for r in range(3)]
         ident = held.tile([P, P], F32, name="ident", align_bytes=64)
         hq = [held.tile([P, 2 * C], U32, name="hq%d" % g, align_bytes=64) for g in range(PAIRS)]
         hs = [held.tile([P, 2 * C], U8, name="hs%d" % g, align_bytes=64) for g in range(PAIRS)]
@@ -75,13 +76,16 @@ def tile_moe_cpy_mlp_gelu_kernel(
         for b in range(BLOCKS):
             nc.vector.memset(ys[b][:, SLOTS + T :], 0.0)
 
+        warm = held.tile([P, 1], F32, name="warm")
+        nc.scalar.activation(warm[:], ys[0][:, WIDE - 1 :], GELU)
+        nc.gpsimd.memset(gate_rows[:], 0.0)
         make_identity(nc, ident[:])
 
-        nc.sync.dma_start(slot_list[:], offs)
-        for q in range(4):
-            queue = nc.sync if q < 2 else nc.scalar
-            queue.dma_start(xs[32 * q : 32 * q + 4, :].bitcast(I32), x_scales[0, 4 * q : 4 * q + 4, :].bitcast(I32))
         nc.sync.dma_start(xw[:].bitcast(I32), x_words[0].rearrange("p t d -> p (t d)").bitcast(I32))
+        for q in range(4):
+            nc.sync.dma_start(xs[32 * q : 32 * q + 4, :].bitcast(I32), x_scales[0, 4 * q : 4 * q + 4, :].bitcast(I32))
+        nc.sync.dma_start(slot_list[:], offs)
+        nc.sync.dma_start(gate_rows[0:4, :], gate.rearrange("r p t -> (r p) t")[0 : 3 * P : P - 1, :])
         for i, (lo, hi) in enumerate(W1_LOADS):
             load_words(w1[:, lo:hi, :], w1_words[lo:hi, 0])
             if i == 0:
@@ -92,10 +96,8 @@ def tile_moe_cpy_mlp_gelu_kernel(
         load_words(w2a[:], w2_words[:, 0, :, 0:P, :])
         load_xr(0)
         nc.sync.dma_start(choice_lists[0][:], pos1)
-        nc.sync.dma_start(gate1[:], gate[0])
         nc.sync.dma_start(choice_lists[1][:], pos2)
         nc.sync.dma_start(choice_lists[2][:], pos3)
-        nc.sync.dma_start(gate23[:], gate[1:3].rearrange("r p t -> p r t"))
         load_words(w2b[:], w2_words[:, 0, :, P : 2 * P, :])
         load_xr(1)
         load_words(w2c[:], w2_words[:, 0, :, 2 * P :, :])
@@ -116,29 +118,53 @@ def tile_moe_cpy_mlp_gelu_kernel(
             nc.vector.tensor_copy(xg[g][:], xw[:].indirect(picks))
             nc.vector.tensor_copy(xgs[g][:], xs[:].indirect(picks))
 
+        def gate_columns():
+            for i, (lo, hi) in enumerate(HALVES):
+                flipped = psum.tile([P, 3, P], F32, name="flipped", tag="bank%d" % (3 + i))
+                for j in range(lo, hi):
+                    nc.tensor.transpose(flipped[:, j - lo, :], gate_rows[:, j * P : (j + 1) * P], ident[:])
+                nc.scalar.copy(gate_cols[:, lo:hi, :], flipped[:, : hi - lo, 0:4])
+
+        def spread_gate(r, banks):
+            for i, (lo, hi) in enumerate(HALVES):
+                spread = psum.tile([P, 3 * P], F32, name="spread", tag="bank%d" % banks[i])
+                for j in range(lo, hi):
+                    nc.tensor.transpose(
+                        spread[:, (j - lo) * P : (j - lo + 1) * P],
+                        gate_cols[:, j, r + 1 : r + 2].to_broadcast([P, P]),
+                        ident[:],
+                    )
+                nc.scalar.copy(gates[r][:, lo * P : hi * P], spread[:, : (hi - lo) * P])
+
+        h_rows = {}
+
         def first_layer(g):
-            turned = psum.tile([P, 2, 2, C], F32, name="turned", tag="bank%d" % (3 + g % 3))
-            for a in range(2):
-                e = 2 * g + a
-                pre = psum.tile([P, H], F32, name="pre", tag="bank%d" % (e % 3))
-                nc.tensor.matmul_mx(
-                    out=pre[:],
-                    lhsT=xg[g][:, a * C : (a + 1) * C].bitcast(FP8X4),
-                    lhsT_scale=xgs[g][:, a * C : (a + 1) * C],
-                    rhs=w1[:, e, :].bitcast(FP8X4),
-                    rhs_scale=w1s[:, e, :],
-                    start=True,
-                    stop=True,
-                )
-                h_rows = ring.tile([P, H], BF16, name="h_rows", tag="h_rows", bufs=4, align_bytes=64)
+            h_rows[g] = ring.tile([P, 2, 2, P, 2], BF16, name="h_rows", tag="h_rows", bufs=3, align_bytes=64)
+            for half in range(2):
+                pre = psum.tile([P, 2, H // 2], F32, name="pre", tag="bank%d" % PRE_BANKS[g % 2][half])
+                cols = slice(half * H // 2, (half + 1) * H // 2)
+                for a in range(2):
+                    nc.tensor.matmul_mx(
+                        out=pre[:, a, :],
+                        lhsT=xg[g][:, a * C : (a + 1) * C].bitcast(FP8X4),
+                        lhsT_scale=xgs[g][:, a * C : (a + 1) * C],
+                        rhs=w1[:, 2 * g + a, cols].bitcast(FP8X4),
+                        rhs_scale=w1s[:, 2 * g + a, cols],
+                        start=True,
+                        stop=True,
+                    )
                 nc.scalar.activation(
-                    h_rows[:].rearrange("s (u p d) -> s u p d", u=2, d=2),
-                    pre[:].rearrange("s (p u d) -> s u p d", u=2, d=2),
+                    h_rows[g][:, :, :, half * P // 2 : (half + 1) * P // 2, :],
+                    pre[:].rearrange("s a (p u d) -> s u a p d", u=2, d=2),
                     GELU,
                 )
-                pairs = h_rows[:].bitcast(F32)
+
+        def turn_and_quantise(g):
+            turned = psum.tile([P, 2, 2, C], F32, name="turned", tag="bank%d" % (3 + g % 3))
+            pairs = h_rows[g][:].rearrange("s u a p d -> s (u a p d)").bitcast(F32)
+            for a in range(2):
                 for u in range(2):
-                    nc.tensor.transpose(turned[:, a, u, :], pairs[:, u * P : (u + 1) * P], ident[:])
+                    nc.tensor.transpose(turned[:, a, u, :], pairs[:, (2 * u + a) * P : (2 * u + a + 1) * P], ident[:])
             h_cols = ring.tile([P, 2 * C * 4], BF16, name="h_cols", tag="h_cols", bufs=5, align_bytes=64)
             dst = h_cols[:].bitcast(F32).rearrange("p (a s u) -> p a s u", a=2, u=2)
             src = turned[:].rearrange("p a u s -> p a s u")
@@ -147,6 +173,34 @@ def tile_moe_cpy_mlp_gelu_kernel(
             else:
                 nc.vector.tensor_copy(dst, src)
             nc.vector.quantize_mx(out=hq[g][:].bitcast(FP8X4), scales=hs[g][:], in_=h_cols[:])
+
+        def lone_first_layer(e):
+            g, a = divmod(e, 2)
+            h_rows[e] = ring.tile([P, 2, P, 2], BF16, name="h_lone", tag="h_lone", bufs=2, align_bytes=64)
+            pre = psum.tile([P, H], F32, name="pre", tag="bank%d" % PRE_BANKS[g % 2][a])
+            nc.tensor.matmul_mx(
+                out=pre[:],
+                lhsT=xg[g][:, a * C : (a + 1) * C].bitcast(FP8X4),
+                lhsT_scale=xgs[g][:, a * C : (a + 1) * C],
+                rhs=w1[:, e, :].bitcast(FP8X4),
+                rhs_scale=w1s[:, e, :],
+                start=True,
+                stop=True,
+            )
+            nc.scalar.activation(h_rows[e][:], pre[:].rearrange("s (p u d) -> s u p d", u=2, d=2), GELU)
+
+        def lone_turn_and_quantise(e):
+            g, a = divmod(e, 2)
+            turned = psum.tile([P, 2, C], F32, name="turned", tag="bank%d" % (4 + a))
+            pairs = h_rows[e][:].rearrange("s u p d -> s (u p d)").bitcast(F32)
+            for u in range(2):
+                nc.tensor.transpose(turned[:, u, :], pairs[:, u * P : (u + 1) * P], ident[:])
+            h_cols = ring.tile([P, C * 4], BF16, name="h_cols_lone", tag="h_cols_lone", bufs=2, align_bytes=64)
+            nc.vector.tensor_copy(
+                h_cols[:].bitcast(F32).rearrange("p (s u) -> p s u", u=2), turned[:].rearrange("p u s -> p s u")
+            )
+            cols = slice(a * C, (a + 1) * C)
+            nc.vector.quantize_mx(out=hq[g][:, cols].bitcast(FP8X4), scales=hs[g][:, cols], in_=h_cols[:])
 
         def second_layer(b, i):
             lo, hi = GROUPS[i]
@@ -194,14 +248,27 @@ def tile_moe_cpy_mlp_gelu_kernel(
                 nc.scalar.copy(result[:, lo * P : hi * P], back[:, : n * P])
             nc.sync.dma_start(out[b * P : (b + 1) * P, :], result[:])
 
-        for g in range(PAIRS):
-            first_layer(g)
-        for i in range(len(GROUPS)):
-            second_layer(0, i)
+        gate_columns()
+        spread_gate(0, (5, 6))
+        first_layer(0)
+        for g in range(PAIRS - 1):
+            if g + 1 < PAIRS - 1:
+                first_layer(g + 1)
+            else:
+                lone_first_layer(E - 2)
+                lone_first_layer(E - 1)
+            turn_and_quantise(g)
+        lone_turn_and_quantise(E - 2)
+        second_layer(0, 0)
+        second_layer(0, 1)
+        lone_turn_and_quantise(E - 1)
+        second_layer(0, 2)
+        spread_gate(1, (0, 1))
+        spread_gate(2, (2, 0))
         for b in range(BLOCKS - 1):
             for i in range(len(GROUPS)):
                 second_layer(b + 1, i)
-            terms = [weighted(b, r, 0, T, "term", 6) for r in range(3)]
+            terms = [weighted(b, r, 0, T, "term", 9) for r in range(3)]
             summed_on_tensor(b, terms)
 
         b = BLOCKS - 1

@@ -63,36 +63,34 @@ def tile_moe_cpy_mlp_gelu_kernel(
         def load_words(tile, words):
             nc.sync.dma_start(tile.bitcast(I32), words.rearrange("e p n d -> p e (n d)").bitcast(I32))
 
-        def load_scales(queue, plane, row, scales, q):
-            queue.dma_start(
-                plane[32 * q + row : 32 * q + row + 4].bitcast(I32),
-                scales[:, 0, 4 * q : 4 * q + 4, :].rearrange("e r n -> r e n").bitcast(I32),
-            )
+        def load_scales(plane, row, scales):
+            for r in range(4):
+                nc.gpsimd.dma_start(
+                    plane[row + r : P : 32].bitcast(I32),
+                    scales[:, 0, r:16:4, :].rearrange("e q n -> q e n").bitcast(I32),
+                )
 
         def load_xr(b):
             nc.sync.dma_start(ys[b][:, SLOTS : SLOTS + T], xr[b * P : (b + 1) * P, :])
 
         nc.vector.memset(xs[:].bitcast(I32), 0)
+        nc.vector.memset(gate_rows[:], 0.0)
         for b in range(BLOCKS):
             nc.vector.memset(ys[b][:, SLOTS + T :], 0.0)
 
         warm = held.tile([P, 1], F32, name="warm")
         nc.scalar.activation(warm[:], ys[0][:, WIDE - 1 :], GELU)
-        nc.gpsimd.memset(gate_rows[:], 0.0)
+        load_scales(w1s, 0, w1_scales)
         make_identity(nc, ident[:])
+        load_scales(w2s, W2_ROW, w2_scales)
 
         nc.sync.dma_start(xw[:].bitcast(I32), x_words[0].rearrange("p t d -> p (t d)").bitcast(I32))
-        for q in range(4):
-            nc.sync.dma_start(xs[32 * q : 32 * q + 4, :].bitcast(I32), x_scales[0, 4 * q : 4 * q + 4, :].bitcast(I32))
+        for r in range(4):
+            nc.sync.dma_start(xs[r:P:32, :].bitcast(I32), x_scales[0, r:16:4, :].bitcast(I32))
         nc.sync.dma_start(slot_list[:], offs)
         nc.sync.dma_start(gate_rows[0:4, :], gate.rearrange("r p t -> (r p) t")[0 : 3 * P : P - 1, :])
-        for i, (lo, hi) in enumerate(W1_LOADS):
+        for lo, hi in W1_LOADS:
             load_words(w1[:, lo:hi, :], w1_words[lo:hi, 0])
-            if i == 0:
-                for q in range(4):
-                    load_scales(nc.sync, w1s, 0, w1_scales, q)
-        for q in range(4):
-            load_scales(nc.sync, w2s, W2_ROW, w2_scales, q)
         load_words(w2a[:], w2_words[:, 0, :, 0:P, :])
         load_xr(0)
         nc.sync.dma_start(choice_lists[0][:], pos1)

@@ -25,7 +25,8 @@ PAIRS = E // 2
 BLOCKS = K // P
 W2_ROW = 4
 GROUPS = ((0, 4), (4, 8), (8, 10))
-SHARED = ((6, 7, 5), (6, 3, 4))
+FILL_BANKS = ((0, 1, 5), (5, 6, 6), (6, 5, 5), (5, 6, 6))
+QUADRANTS = (0, 2, 1, 3)
 W1_LOADS = ((0, 2), (2, 4), (4, 6), (6, 8), (8, 10))
 PRE_BANKS = ((0, 1), (2, 7))
 HALVES = ((0, 3), (3, 5))
@@ -54,7 +55,7 @@ def tile_moe_cpy_mlp_gelu_kernel(
         w2c = held.tile([P, E, 2 * P], U32, name="w2c", align_bytes=64)
         ys = [held.tile([P, WIDE], F32, name="y%d" % b, align_bytes=64) for b in range(BLOCKS)]
         gate_rows = held.tile([P, T], F32, name="gate_rows", align_bytes=64)
-        gate_cols = held.tile([P, T // P, 4], F32, name="gate_cols", align_bytes=64)
+        gate_cols = held.tile([P, T // P, 2], F32, name="gate_cols", align_bytes=64)
         gates = [held.tile([P, T], F32, name="gate%d" % r, align_bytes=64) for r in range(3)]
         ident = held.tile([P, P], F32, name="ident", align_bytes=64)
         hq = [held.tile([P, 2 * C], U32, name="hq%d" % g, align_bytes=64) for g in range(PAIRS)]
@@ -64,10 +65,10 @@ def tile_moe_cpy_mlp_gelu_kernel(
             nc.sync.dma_start(tile.bitcast(I32), words.rearrange("e p n d -> p e (n d)").bitcast(I32))
 
         def load_scales(plane, row, scales):
-            for r in range(4):
-                nc.gpsimd.dma_start(
-                    plane[row + r : P : 32].bitcast(I32),
-                    scales[:, 0, r:16:4, :].rearrange("e q n -> q e n").bitcast(I32),
+            for q in QUADRANTS:
+                nc.sync.dma_start(
+                    plane[32 * q + row : 32 * q + row + 4].bitcast(I32),
+                    scales[:, 0, 4 * q : 4 * q + 4, :].rearrange("e r n -> r e n").bitcast(I32),
                 )
 
         def load_xr(b):
@@ -80,20 +81,22 @@ def tile_moe_cpy_mlp_gelu_kernel(
 
         warm = held.tile([P, 1], F32, name="warm")
         nc.scalar.activation(warm[:], ys[0][:, WIDE - 1 :], GELU)
-        load_scales(w1s, 0, w1_scales)
         make_identity(nc, ident[:])
-        load_scales(w2s, W2_ROW, w2_scales)
 
         nc.sync.dma_start(xw[:].bitcast(I32), x_words[0].rearrange("p t d -> p (t d)").bitcast(I32))
-        for r in range(4):
-            nc.sync.dma_start(xs[r:P:32, :].bitcast(I32), x_scales[0, r:16:4, :].bitcast(I32))
+        for q in QUADRANTS:
+            nc.sync.dma_start(xs[32 * q : 32 * q + 4, :].bitcast(I32), x_scales[0, 4 * q : 4 * q + 4, :].bitcast(I32))
         nc.sync.dma_start(slot_list[:], offs)
-        nc.sync.dma_start(gate_rows[0:4, :], gate.rearrange("r p t -> (r p) t")[0 : 3 * P : P - 1, :])
         for lo, hi in W1_LOADS:
             load_words(w1[:, lo:hi, :], w1_words[lo:hi, 0])
+            if lo == 0:
+                load_scales(w1s, 0, w1_scales)
+        load_scales(w2s, W2_ROW, w2_scales)
+        nc.sync.dma_start(gate_rows[0:2, :], gate[1:3, 0, :])
         load_words(w2a[:], w2_words[:, 0, :, 0:P, :])
         load_xr(0)
         nc.sync.dma_start(choice_lists[0][:], pos1)
+        nc.sync.dma_start(gates[0][:], gate[0])
         nc.sync.dma_start(choice_lists[1][:], pos2)
         nc.sync.dma_start(choice_lists[2][:], pos3)
         load_words(w2b[:], w2_words[:, 0, :, P : 2 * P, :])
@@ -118,10 +121,10 @@ def tile_moe_cpy_mlp_gelu_kernel(
 
         def gate_columns():
             for i, (lo, hi) in enumerate(HALVES):
-                flipped = psum.tile([P, 3, P], F32, name="flipped", tag="bank%d" % (3 + i))
+                flipped = psum.tile([P, 3, P], F32, name="flipped", tag="bank%d" % (2, 7)[i])
                 for j in range(lo, hi):
                     nc.tensor.transpose(flipped[:, j - lo, :], gate_rows[:, j * P : (j + 1) * P], ident[:])
-                nc.scalar.copy(gate_cols[:, lo:hi, :], flipped[:, : hi - lo, 0:4])
+                nc.scalar.copy(gate_cols[:, lo:hi, :], flipped[:, : hi - lo, 0:2])
 
         def spread_gate(r, banks):
             for i, (lo, hi) in enumerate(HALVES):
@@ -129,7 +132,7 @@ def tile_moe_cpy_mlp_gelu_kernel(
                 for j in range(lo, hi):
                     nc.tensor.transpose(
                         spread[:, (j - lo) * P : (j - lo + 1) * P],
-                        gate_cols[:, j, r + 1 : r + 2].to_broadcast([P, P]),
+                        gate_cols[:, j, r - 1 : r].to_broadcast([P, P]),
                         ident[:],
                     )
                 nc.scalar.copy(gates[r][:, lo * P : hi * P], spread[:, : (hi - lo) * P])
@@ -202,8 +205,8 @@ def tile_moe_cpy_mlp_gelu_kernel(
 
         def second_layer(b, i):
             lo, hi = GROUPS[i]
-            acc = psum.tile([P, 4 * C], F32, name="acc", tag="bank%d" % SHARED[b % 2][i])
-            for e in range(lo, hi):
+            acc = psum.tile([P, 4 * C], F32, name="acc", tag="bank%d" % FILL_BANKS[b][i])
+            for e in (range(lo, hi) if b == 0 else reversed(range(lo, hi))):
                 cols = slice((e % 2) * C, (e % 2 + 1) * C)
                 nc.tensor.matmul_mx(
                     out=acc[:, (e - lo) * C : (e - lo + 1) * C],
@@ -227,7 +230,7 @@ def tile_moe_cpy_mlp_gelu_kernel(
             result = ring.tile([P, T], F32, name="result", tag="result", bufs=2, align_bytes=64)
             for i, (lo, hi) in enumerate(HALVES):
                 n = hi - lo
-                total = psum.tile([P, 3 * P], F32, name="total", tag="bank%d" % SHARED[(b + 1) % 2][i + 1])
+                total = psum.tile([P, 3 * P], F32, name="total", tag="bank%d" % (5 + i))
                 for j in range(lo, hi):
                     for r in range(3):
                         nc.tensor.matmul(
@@ -244,10 +247,8 @@ def tile_moe_cpy_mlp_gelu_kernel(
                 for j in range(n):
                     nc.tensor.transpose(back[:, j * P : (j + 1) * P], by_token[:, j * P : (j + 1) * P], ident[:])
                 nc.scalar.copy(result[:, lo * P : hi * P], back[:, : n * P])
-            nc.sync.dma_start(out[b * P : (b + 1) * P, :], result[:])
+            nc.scalar.dma_start(out[b * P : (b + 1) * P, :], result[:])
 
-        gate_columns()
-        spread_gate(0, (5, 6))
         first_layer(0)
         for g in range(PAIRS - 1):
             if g + 1 < PAIRS - 1:
@@ -258,32 +259,31 @@ def tile_moe_cpy_mlp_gelu_kernel(
             turn_and_quantise(g)
         lone_turn_and_quantise(E - 2)
         second_layer(0, 0)
-        second_layer(0, 1)
         lone_turn_and_quantise(E - 1)
+        second_layer(0, 1)
         second_layer(0, 2)
-        spread_gate(1, (0, 1))
-        spread_gate(2, (2, 0))
+        gate_columns()
+        spread_gate(1, (2, 7))
+        spread_gate(2, (6, 5))
+        for b in range(1, BLOCKS):
+            for i in (2, 0, 1):
+                second_layer(b, i)
         for b in range(BLOCKS - 1):
-            for i in range(len(GROUPS)):
-                second_layer(b + 1, i)
-            terms = [weighted(b, r, 0, T, "term", 9) for r in range(3)]
-            summed_on_tensor(b, terms)
+            summed_on_tensor(b, [weighted(b, r, 0, T, "term", 9) for r in range(3)])
 
-        b = BLOCKS - 1
+        def added(x, y, tag, bufs):
+            both = ring.tile(list(x.shape), F32, name="both", tag=tag, bufs=bufs, align_bytes=64)
+            nc.vector.tensor_tensor(both[:], x[:], y[:], ADD)
+            return both
+
         half = T // 2
-        a0 = weighted(b, 0, 0, half, "last", 10)
-        b0 = weighted(b, 1, 0, half, "last", 10)
-        a1 = weighted(b, 0, half, T, "last", 10)
-        ab0 = ring.tile([P, half], F32, name="ab0", tag="last", bufs=10, align_bytes=64)
-        nc.vector.tensor_tensor(ab0[:], a0[:], b0[:], ADD)
-        c0 = weighted(b, 2, 0, half, "last", 10)
-        b1 = weighted(b, 1, half, T, "last", 10)
-        abc0 = ring.tile([P, half], F32, name="abc0", tag="last", bufs=10, align_bytes=64)
-        nc.vector.tensor_tensor(abc0[:], ab0[:], c0[:], ADD)
-        nc.sync.dma_start(out[b * P : (b + 1) * P, :half], abc0[:])
-        ab1 = ring.tile([P, half], F32, name="ab1", tag="last", bufs=10, align_bytes=64)
-        nc.vector.tensor_tensor(ab1[:], a1[:], b1[:], ADD)
-        c1 = weighted(b, 2, half, T, "last", 10)
-        abc1 = ring.tile([P, half], F32, name="abc1", tag="last", bufs=10, align_bytes=64)
-        nc.vector.tensor_tensor(abc1[:], ab1[:], c1[:], ADD)
-        nc.sync.dma_start(out[b * P : (b + 1) * P, half:], abc1[:])
+        a0 = weighted(3, 0, 0, half, "last", 10)
+        b0 = weighted(3, 1, 0, half, "last", 10)
+        a1 = weighted(3, 0, half, T, "last", 10)
+        ab0 = added(a0, b0, "last", 10)
+        c0 = weighted(3, 2, 0, half, "last", 10)
+        b1 = weighted(3, 1, half, T, "last", 10)
+        nc.sync.dma_start(out[3 * P :, :half], added(ab0, c0, "last", 10)[:])
+        ab1 = added(a1, b1, "last", 10)
+        c1 = weighted(3, 2, half, T, "last", 10)
+        nc.sync.dma_start(out[3 * P :, half:], added(ab1, c1, "last", 10)[:])

@@ -26,7 +26,6 @@ BLOCKS = K // P
 W2_ROW = 4
 GROUPS = ((0, 4), (4, 8), (8, 10))
 FILL_BANKS = ((0, 1, 5), (5, 6, 6), (6, 5, 5), (5, 6, 6))
-QUADRANTS = (0, 2, 1, 3)
 W1_LOADS = ((0, 2), (2, 4), (4, 6), (6, 8), (8, 10))
 PRE_BANKS = ((0, 1), (2, 7))
 HALVES = ((0, 3), (3, 5))
@@ -50,9 +49,7 @@ def tile_moe_cpy_mlp_gelu_kernel(
         w1 = held.tile([P, E, H], U32, name="w1", align_bytes=64)
         w1s = held.tile([P, E, H], U8, name="w1s", align_bytes=64)
         w2s = held.tile([P, E, K], U8, name="w2s", align_bytes=64)
-        w2a = held.tile([P, E, P], U32, name="w2a", align_bytes=64)
-        w2b = held.tile([P, E, P], U32, name="w2b", align_bytes=64)
-        w2c = held.tile([P, E, 2 * P], U32, name="w2c", align_bytes=64)
+        w2 = [held.tile([P, E, P], U32, name="w2_%d" % b, align_bytes=64) for b in range(BLOCKS)]
         ys = [held.tile([P, WIDE], F32, name="y%d" % b, align_bytes=64) for b in range(BLOCKS)]
         gate_rows = held.tile([P, T], F32, name="gate_rows", align_bytes=64)
         gate_cols = held.tile([P, T // P, 2], F32, name="gate_cols", align_bytes=64)
@@ -65,11 +62,14 @@ def tile_moe_cpy_mlp_gelu_kernel(
             nc.sync.dma_start(tile.bitcast(I32), words.rearrange("e p n d -> p e (n d)").bitcast(I32))
 
         def load_scales(plane, row, scales):
-            for q in QUADRANTS:
+            for r in range(4):
                 nc.sync.dma_start(
-                    plane[32 * q + row : 32 * q + row + 4].bitcast(I32),
-                    scales[:, 0, 4 * q : 4 * q + 4, :].rearrange("e r n -> r e n").bitcast(I32),
+                    plane[row + r : P : 32].bitcast(I32),
+                    scales[:, 0, r:16:4, :].rearrange("e q n -> q e n").bitcast(I32),
                 )
+
+        def load_w2(b):
+            load_words(w2[b][:], w2_words[:, 0, :, b * P : (b + 1) * P, :])
 
         def load_xr(b):
             nc.sync.dma_start(ys[b][:, SLOTS : SLOTS + T], xr[b * P : (b + 1) * P, :])
@@ -84,7 +84,7 @@ def tile_moe_cpy_mlp_gelu_kernel(
         make_identity(nc, ident[:])
 
         nc.sync.dma_start(xw[:].bitcast(I32), x_words[0].rearrange("p t d -> p (t d)").bitcast(I32))
-        for q in QUADRANTS:
+        for q in range(4):
             nc.sync.dma_start(xs[32 * q : 32 * q + 4, :].bitcast(I32), x_scales[0, 4 * q : 4 * q + 4, :].bitcast(I32))
         nc.sync.dma_start(slot_list[:], offs)
         for lo, hi in W1_LOADS:
@@ -93,24 +93,15 @@ def tile_moe_cpy_mlp_gelu_kernel(
                 load_scales(w1s, 0, w1_scales)
         load_scales(w2s, W2_ROW, w2_scales)
         nc.sync.dma_start(gate_rows[0:2, :], gate[1:3, 0, :])
-        load_words(w2a[:], w2_words[:, 0, :, 0:P, :])
+        load_w2(0)
         load_xr(0)
         nc.sync.dma_start(choice_lists[0][:], pos1)
         nc.sync.dma_start(gates[0][:], gate[0])
         nc.sync.dma_start(choice_lists[1][:], pos2)
         nc.sync.dma_start(choice_lists[2][:], pos3)
-        load_words(w2b[:], w2_words[:, 0, :, P : 2 * P, :])
-        load_xr(1)
-        load_words(w2c[:], w2_words[:, 0, :, 2 * P :, :])
-        load_xr(2)
-        load_xr(3)
-
-        def w2_codes(e, b):
-            if b == 0:
-                return w2a[:, e, :]
-            if b == 1:
-                return w2b[:, e, :]
-            return w2c[:, e, (b - 2) * P : (b - 1) * P]
+        for b in range(1, BLOCKS):
+            load_w2(b)
+            load_xr(b)
 
         xg = [held.tile([P, 2 * C], U32, name="xg%d" % g, align_bytes=64) for g in range(PAIRS)]
         xgs = [held.tile([P, 2 * C], U8, name="xgs%d" % g, align_bytes=64) for g in range(PAIRS)]
@@ -210,7 +201,7 @@ def tile_moe_cpy_mlp_gelu_kernel(
                 cols = slice((e % 2) * C, (e % 2 + 1) * C)
                 nc.tensor.matmul_mx(
                     out=acc[:, (e - lo) * C : (e - lo + 1) * C],
-                    lhsT=w2_codes(e, b).bitcast(FP8X4),
+                    lhsT=w2[b][:, e, :].bitcast(FP8X4),
                     lhsT_scale=w2s[W2_ROW:, e, b * P : (b + 1) * P],
                     rhs=hq[e // 2][:, cols].bitcast(FP8X4),
                     rhs_scale=hs[e // 2][:, cols],
@@ -230,7 +221,7 @@ def tile_moe_cpy_mlp_gelu_kernel(
             result = ring.tile([P, T], F32, name="result", tag="result", bufs=2, align_bytes=64)
             for i, (lo, hi) in enumerate(HALVES):
                 n = hi - lo
-                total = psum.tile([P, 3 * P], F32, name="total", tag="bank%d" % (5 + i))
+                total = psum.tile([P, 3 * P], F32, name="total", tag="bank%d" % FILL_BANKS[2 if b == 0 else 3][i])
                 for j in range(lo, hi):
                     for r in range(3):
                         nc.tensor.matmul(
@@ -266,9 +257,11 @@ def tile_moe_cpy_mlp_gelu_kernel(
         spread_gate(1, (2, 7))
         spread_gate(2, (6, 5))
         for b in range(1, BLOCKS):
+            if b == BLOCKS - 1:
+                summed_on_tensor(0, [weighted(0, r, 0, T, "term", 9) for r in range(3)])
             for i in (2, 0, 1):
                 second_layer(b, i)
-        for b in range(BLOCKS - 1):
+        for b in range(1, BLOCKS - 1):
             summed_on_tensor(b, [weighted(b, r, 0, T, "term", 9) for r in range(3)])
 
         def added(x, y, tag, bufs):

@@ -25,10 +25,13 @@ PAIRS = E // 2
 BLOCKS = K // P
 W2_ROW = 4
 GROUPS = ((0, 4), (4, 8), (8, 10))
-FILL_BANKS = ((0, 1, 5), (5, 6, 6), (6, 5, 5), (5, 6, 6))
-W1_LOADS = ((0, 2), (2, 4), (4, 6), (6, 8), (8, 10))
+FIRST_FILL_BANKS = (1, 0, 2)
+FILL_BANKS = (6, 7, 2)
+W1_LOADS = ((0, 2), (2, 4), (4, 6), (6, 8), (8, 9), (9, 10))
 PRE_BANKS = ((0, 1), (2, 7))
 HALVES = ((0, 3), (3, 5))
+CHUNKS = T // P
+LAST_CUTS = (2 * P, 4 * P)
 
 
 def tile_moe_cpy_mlp_gelu_kernel(
@@ -48,11 +51,17 @@ def tile_moe_cpy_mlp_gelu_kernel(
         xs = held.tile([P, T], U8, name="xs", align_bytes=64)
         w1 = held.tile([P, E, H], U32, name="w1", align_bytes=64)
         w1s = held.tile([P, E, H], U8, name="w1s", align_bytes=64)
-        w2s = held.tile([P, E, K], U8, name="w2s", align_bytes=64)
-        w2 = [held.tile([P, E, P], U32, name="w2_%d" % b, align_bytes=64) for b in range(BLOCKS)]
+        w2s_first = held.tile([P, E, P], U8, name="w2s_first", align_bytes=64)
+        w2s_rest = held.tile([P, E, K - P], U8, name="w2s_rest", align_bytes=64)
+        w2 = [
+            [held.tile([P, hi - lo, P], U32, name="w2_%d_%d" % (b, i), align_bytes=64) for i, (lo, hi) in enumerate(GROUPS)]
+            for b in range(2)
+        ]
+        for b in range(2, BLOCKS):
+            whole = held.tile([P, E, P], U32, name="w2_%d" % b, align_bytes=64)
+            w2.append([whole[:, lo:hi, :] for lo, hi in GROUPS] + [whole])
         ys = [held.tile([P, WIDE], F32, name="y%d" % b, align_bytes=64) for b in range(BLOCKS)]
-        gate_rows = held.tile([P, T], F32, name="gate_rows", align_bytes=64)
-        gate_cols = held.tile([P, T // P, 2], F32, name="gate_cols", align_bytes=64)
+        gate_rows = held.tile([P, P], F32, name="gate_rows", align_bytes=64)
         gates = [held.tile([P, T], F32, name="gate%d" % r, align_bytes=64) for r in range(3)]
         ident = held.tile([P, P], F32, name="ident", align_bytes=64)
         hq = [held.tile([P, 2 * C], U32, name="hq%d" % g, align_bytes=64) for g in range(PAIRS)]
@@ -61,21 +70,22 @@ def tile_moe_cpy_mlp_gelu_kernel(
         def load_words(tile, words):
             nc.sync.dma_start(tile.bitcast(I32), words.rearrange("e p n d -> p e (n d)").bitcast(I32))
 
-        def load_scales(plane, row, scales):
-            for r in range(4):
-                nc.sync.dma_start(
+        def load_scales(queue, plane, row, scales, rows):
+            for r in rows:
+                queue.dma_start(
                     plane[row + r : P : 32].bitcast(I32),
                     scales[:, 0, r:16:4, :].rearrange("e q n -> q e n").bitcast(I32),
                 )
 
         def load_w2(b):
-            load_words(w2[b][:], w2_words[:, 0, :, b * P : (b + 1) * P, :])
+            load_words(w2[b][3][:], w2_words[:, 0, :, b * P : (b + 1) * P, :])
 
         def load_xr(b):
             nc.sync.dma_start(ys[b][:, SLOTS : SLOTS + T], xr[b * P : (b + 1) * P, :])
 
-        nc.vector.memset(xs[:].bitcast(I32), 0)
-        nc.vector.memset(gate_rows[:], 0.0)
+        nc.gpsimd.memset(xs[:].bitcast(I32), 0)
+        nc.gpsimd.memset(gate_rows[:], 0.0)
+        nc.gpsimd.dma_start(gate_rows[0 : 2 * CHUNKS], gate[1:3, 0, :].rearrange("r (j p) -> r j p", p=P))
         for b in range(BLOCKS):
             nc.vector.memset(ys[b][:, SLOTS + T :], 0.0)
 
@@ -90,16 +100,20 @@ def tile_moe_cpy_mlp_gelu_kernel(
         for lo, hi in W1_LOADS:
             load_words(w1[:, lo:hi, :], w1_words[lo:hi, 0])
             if lo == 0:
-                load_scales(w1s, 0, w1_scales)
-        load_scales(w2s, W2_ROW, w2_scales)
-        nc.sync.dma_start(gate_rows[0:2, :], gate[1:3, 0, :])
-        load_w2(0)
-        load_xr(0)
+                load_scales(nc.sync, w1s, 0, w1_scales, range(4))
+        load_scales(nc.sync, w2s_first, W2_ROW, w2_scales[:, :, :, :P], range(4))
+        for i, (lo, hi) in enumerate(GROUPS):
+            load_words(w2[0][i][:], w2_words[lo:hi, 0, :, 0:P, :])
         nc.sync.dma_start(choice_lists[0][:], pos1)
+        load_xr(0)
         nc.sync.dma_start(gates[0][:], gate[0])
         nc.sync.dma_start(choice_lists[1][:], pos2)
         nc.sync.dma_start(choice_lists[2][:], pos3)
-        for b in range(1, BLOCKS):
+        load_scales(nc.sync, w2s_rest, W2_ROW, w2_scales[:, :, :, P:], range(4))
+        for i, (lo, hi) in enumerate(GROUPS):
+            load_words(w2[1][i][:], w2_words[lo:hi, 0, :, P : 2 * P, :])
+        load_xr(1)
+        for b in range(2, BLOCKS):
             load_w2(b)
             load_xr(b)
 
@@ -110,20 +124,13 @@ def tile_moe_cpy_mlp_gelu_kernel(
             nc.vector.tensor_copy(xg[g][:], xw[:].indirect(picks))
             nc.vector.tensor_copy(xgs[g][:], xs[:].indirect(picks))
 
-        def gate_columns():
-            for i, (lo, hi) in enumerate(HALVES):
-                flipped = psum.tile([P, 3, P], F32, name="flipped", tag="bank%d" % (2, 7)[i])
-                for j in range(lo, hi):
-                    nc.tensor.transpose(flipped[:, j - lo, :], gate_rows[:, j * P : (j + 1) * P], ident[:])
-                nc.scalar.copy(gate_cols[:, lo:hi, :], flipped[:, : hi - lo, 0:2])
-
-        def spread_gate(r, banks):
+        def spread_gate(gate_cols, r, banks):
             for i, (lo, hi) in enumerate(HALVES):
                 spread = psum.tile([P, 3 * P], F32, name="spread", tag="bank%d" % banks[i])
                 for j in range(lo, hi):
                     nc.tensor.transpose(
                         spread[:, (j - lo) * P : (j - lo + 1) * P],
-                        gate_cols[:, j, r - 1 : r].to_broadcast([P, P]),
+                        gate_cols[:, (r - 1) * CHUNKS + j : (r - 1) * CHUNKS + j + 1].to_broadcast([P, P]),
                         ident[:],
                     )
                 nc.scalar.copy(gates[r][:, lo * P : hi * P], spread[:, : (hi - lo) * P])
@@ -131,7 +138,7 @@ def tile_moe_cpy_mlp_gelu_kernel(
         h_rows = {}
 
         def first_layer(g):
-            h_rows[g] = ring.tile([P, 2, 2, P, 2], BF16, name="h_rows", tag="h_rows", bufs=3, align_bytes=64)
+            h_rows[g] = ring.tile([P, 2, 2, P, 2], BF16, name="h_rows", tag="h_rows", bufs=4, align_bytes=64)
             for half in range(2):
                 pre = psum.tile([P, 2, H // 2], F32, name="pre", tag="bank%d" % PRE_BANKS[g % 2][half])
                 cols = slice(half * H // 2, (half + 1) * H // 2)
@@ -160,7 +167,7 @@ def tile_moe_cpy_mlp_gelu_kernel(
             h_cols = ring.tile([P, 2 * C * 4], BF16, name="h_cols", tag="h_cols", bufs=5, align_bytes=64)
             dst = h_cols[:].bitcast(F32).rearrange("p (a s u) -> p a s u", a=2, u=2)
             src = turned[:].rearrange("p a u s -> p a s u")
-            if g < 2:
+            if g < 1:
                 nc.scalar.copy(dst, src)
             else:
                 nc.vector.tensor_copy(dst, src)
@@ -187,8 +194,8 @@ def tile_moe_cpy_mlp_gelu_kernel(
             pairs = h_rows[e][:].rearrange("s u p d -> s (u p d)").bitcast(F32)
             for u in range(2):
                 nc.tensor.transpose(turned[:, u, :], pairs[:, u * P : (u + 1) * P], ident[:])
-            h_cols = ring.tile([P, C * 4], BF16, name="h_cols_lone", tag="h_cols_lone", bufs=2, align_bytes=64)
-            nc.vector.tensor_copy(
+            h_cols = ring.tile([P, C * 4], BF16, name="h_cols_lone", tag="h_cols_lone%d" % a, bufs=1, align_bytes=64)
+            nc.scalar.copy(
                 h_cols[:].bitcast(F32).rearrange("p (s u) -> p s u", u=2), turned[:].rearrange("p u s -> p s u")
             )
             cols = slice(a * C, (a + 1) * C)
@@ -196,19 +203,22 @@ def tile_moe_cpy_mlp_gelu_kernel(
 
         def second_layer(b, i):
             lo, hi = GROUPS[i]
-            acc = psum.tile([P, 4 * C], F32, name="acc", tag="bank%d" % FILL_BANKS[b][i])
-            for e in (range(lo, hi) if b == 0 else reversed(range(lo, hi))):
+            acc = psum.tile([P, 4 * C], F32, name="acc", tag="bank%d" % (FILL_BANKS if b else FIRST_FILL_BANKS)[i])
+            for e in range(lo, hi):
                 cols = slice((e % 2) * C, (e % 2 + 1) * C)
                 nc.tensor.matmul_mx(
                     out=acc[:, (e - lo) * C : (e - lo + 1) * C],
-                    lhsT=w2[b][:, e, :].bitcast(FP8X4),
-                    lhsT_scale=w2s[W2_ROW:, e, b * P : (b + 1) * P],
+                    lhsT=w2[b][i][:, e - lo, :].bitcast(FP8X4),
+                    lhsT_scale=w2s_rest[W2_ROW:, e, (b - 1) * P : b * P] if b else w2s_first[W2_ROW:, e, :],
                     rhs=hq[e // 2][:, cols].bitcast(FP8X4),
                     rhs_scale=hs[e // 2][:, cols],
                     start=True,
                     stop=True,
                 )
-            nc.scalar.copy(ys[b][:, lo * C : hi * C], acc[:, : (hi - lo) * C])
+            if (b, i) == (0, 1):
+                nc.vector.tensor_copy(ys[b][:, lo * C : hi * C], acc[:, : (hi - lo) * C])
+            else:
+                nc.scalar.copy(ys[b][:, lo * C : hi * C], acc[:, : (hi - lo) * C])
 
         def weighted(b, r, t0, t1, tag, bufs):
             term = ring.tile([P, t1 - t0], F32, name="term", tag=tag, bufs=bufs, align_bytes=64)
@@ -217,27 +227,35 @@ def tile_moe_cpy_mlp_gelu_kernel(
             )
             return term
 
-        def summed_on_tensor(b, terms):
+        def summed_on_tensor(terms, into, i):
+            n = into.shape[1] // P
+            total = psum.tile([P, 3 * P], F32, name="total", tag="bank%d" % FILL_BANKS[i])
+            for j in range(n):
+                for r in range(3):
+                    nc.tensor.matmul(
+                        total[:, j * P : (j + 1) * P],
+                        lhsT=terms[r][:, j * P : (j + 1) * P],
+                        rhs=ident[:],
+                        is_transpose=True,
+                        start=(r == 0),
+                        stop=(r == 2),
+                    )
+            by_token = ring.tile([P, 3 * P], F32, name="by_token", tag="by_token", bufs=2, align_bytes=64)
+            nc.scalar.copy(by_token[:, : n * P], total[:, : n * P])
+            back = psum.tile([P, 3 * P], F32, name="back", tag="bank%d" % (3 + i))
+            for j in range(n):
+                nc.tensor.transpose(back[:, j * P : (j + 1) * P], by_token[:, j * P : (j + 1) * P], ident[:])
+            nc.scalar.copy(into, back[:, : n * P])
+
+        def combined(b, by_halves):
             result = ring.tile([P, T], F32, name="result", tag="result", bufs=2, align_bytes=64)
+            if by_halves:
+                terms = [[weighted(b, r, lo * P, hi * P, "term", 12)[:] for r in range(3)] for lo, hi in HALVES]
+            else:
+                whole = [weighted(b, r, 0, T, "term", 12) for r in range(3)]
+                terms = [[t[:, lo * P : hi * P] for t in whole] for lo, hi in HALVES]
             for i, (lo, hi) in enumerate(HALVES):
-                n = hi - lo
-                total = psum.tile([P, 3 * P], F32, name="total", tag="bank%d" % FILL_BANKS[2 if b == 0 else 3][i])
-                for j in range(lo, hi):
-                    for r in range(3):
-                        nc.tensor.matmul(
-                            total[:, (j - lo) * P : (j - lo + 1) * P],
-                            lhsT=terms[r][:, j * P : (j + 1) * P],
-                            rhs=ident[:],
-                            is_transpose=True,
-                            start=(r == 0),
-                            stop=(r == 2),
-                        )
-                by_token = ring.tile([P, 3 * P], F32, name="by_token", tag="by_token", bufs=2, align_bytes=64)
-                nc.scalar.copy(by_token[:, : n * P], total[:, : n * P])
-                back = psum.tile([P, 3 * P], F32, name="back", tag="bank%d" % i)
-                for j in range(n):
-                    nc.tensor.transpose(back[:, j * P : (j + 1) * P], by_token[:, j * P : (j + 1) * P], ident[:])
-                nc.scalar.copy(result[:, lo * P : hi * P], back[:, : n * P])
+                summed_on_tensor(terms[i], result[:, lo * P : hi * P], i)
             nc.scalar.dma_start(out[b * P : (b + 1) * P, :], result[:])
 
         first_layer(0)
@@ -248,35 +266,41 @@ def tile_moe_cpy_mlp_gelu_kernel(
                 lone_first_layer(E - 2)
                 lone_first_layer(E - 1)
             turn_and_quantise(g)
+        flipped = psum.tile([P, P], F32, name="flipped", tag="bank7")
+        nc.tensor.transpose(flipped[:], gate_rows[:], ident[:])
         lone_turn_and_quantise(E - 2)
-        second_layer(0, 0)
         lone_turn_and_quantise(E - 1)
+        second_layer(0, 0)
         second_layer(0, 1)
         second_layer(0, 2)
-        gate_columns()
-        spread_gate(1, (2, 7))
-        spread_gate(2, (6, 5))
+        gate_cols = held.tile([P, 2 * CHUNKS], F32, name="gate_cols", tag="w2_0_2", align_bytes=64)
+        nc.scalar.copy(gate_cols[:], flipped[:, 0 : 2 * CHUNKS])
+        spread_gate(gate_cols, 1, (1, 0))
+        spread_gate(gate_cols, 2, (6, 7))
         for b in range(1, BLOCKS):
             if b == BLOCKS - 1:
-                summed_on_tensor(0, [weighted(0, r, 0, T, "term", 9) for r in range(3)])
-            for i in (2, 0, 1):
+                combined(0, False)
+            for i in range(3):
                 second_layer(b, i)
-        for b in range(1, BLOCKS - 1):
-            summed_on_tensor(b, [weighted(b, r, 0, T, "term", 9) for r in range(3)])
+        combined(1, False)
+        combined(2, True)
 
-        def added(x, y, tag, bufs):
-            both = ring.tile(list(x.shape), F32, name="both", tag=tag, bufs=bufs, align_bytes=64)
+        def added(x, y):
+            both = ring.tile(list(x.shape), F32, name="both", tag="last", bufs=10, align_bytes=64)
             nc.vector.tensor_tensor(both[:], x[:], y[:], ADD)
             return both
 
-        half = T // 2
-        a0 = weighted(3, 0, 0, half, "last", 10)
-        b0 = weighted(3, 1, 0, half, "last", 10)
-        a1 = weighted(3, 0, half, T, "last", 10)
-        ab0 = added(a0, b0, "last", 10)
-        c0 = weighted(3, 2, 0, half, "last", 10)
-        b1 = weighted(3, 1, half, T, "last", 10)
-        nc.sync.dma_start(out[3 * P :, :half], added(ab0, c0, "last", 10)[:])
-        ab1 = added(a1, b1, "last", 10)
-        c1 = weighted(3, 2, half, T, "last", 10)
-        nc.sync.dma_start(out[3 * P :, half:], added(ab1, c1, "last", 10)[:])
+        t0, t1 = LAST_CUTS
+        front = ring.tile([P, t0], F32, name="front", tag="result", bufs=2, align_bytes=64)
+        summed_on_tensor([weighted(3, r, 0, t0, "term", 12)[:] for r in range(3)], front[:], 0)
+        nc.scalar.dma_start(out[3 * P :, :t0], front[:])
+        a1 = weighted(3, 0, t0, t1, "last", 10)
+        b1 = weighted(3, 1, t0, t1, "last", 10)
+        a2 = weighted(3, 0, t1, T, "last", 10)
+        ab1 = added(a1, b1)
+        b2 = weighted(3, 1, t1, T, "last", 10)
+        c1 = weighted(3, 2, t0, t1, "last", 10)
+        ab2 = added(a2, b2)
+        c2 = weighted(3, 2, t1, T, "last", 10)
+        nc.sync.dma_start(out[3 * P :, t0:t1], added(ab1, c1)[:])
+        nc.sync.dma_start(out[3 * P :, t1:], added(ab2, c2)[:])

@@ -31,7 +31,7 @@ W1_LOADS = ((0, 2), (2, 4), (4, 6), (6, 8), (8, 9), (9, 10))
 PRE_BANKS = ((0, 1), (2, 7))
 HALVES = ((0, 3), (3, 5))
 CHUNKS = T // P
-LAST_CUTS = (2 * P, 4 * P)
+LAST_CUT = 3 * P
 
 
 def tile_moe_cpy_mlp_gelu_kernel(
@@ -277,12 +277,13 @@ def tile_moe_cpy_mlp_gelu_kernel(
         nc.scalar.copy(gate_cols[:], flipped[:, 0 : 2 * CHUNKS])
         spread_gate(gate_cols, 1, (1, 0))
         spread_gate(gate_cols, 2, (6, 7))
-        for b in range(1, BLOCKS):
-            if b == BLOCKS - 1:
-                combined(0, False)
+        for b in (1, 2):
             for i in range(3):
                 second_layer(b, i)
+        combined(0, False)
         combined(1, False)
+        for i in range(3):
+            second_layer(3, i)
         combined(2, True)
 
         def added(x, y):
@@ -290,17 +291,14 @@ def tile_moe_cpy_mlp_gelu_kernel(
             nc.vector.tensor_tensor(both[:], x[:], y[:], ADD)
             return both
 
-        t0, t1 = LAST_CUTS
-        front = ring.tile([P, t0], F32, name="front", tag="result", bufs=2, align_bytes=64)
-        summed_on_tensor([weighted(3, r, 0, t0, "term", 12)[:] for r in range(3)], front[:], 0)
-        nc.scalar.dma_start(out[3 * P :, :t0], front[:])
-        a1 = weighted(3, 0, t0, t1, "last", 10)
-        b1 = weighted(3, 1, t0, t1, "last", 10)
+        t1 = LAST_CUT
+        a1 = weighted(3, 0, 0, t1, "last", 10)
+        b1 = weighted(3, 1, 0, t1, "last", 10)
         a2 = weighted(3, 0, t1, T, "last", 10)
         ab1 = added(a1, b1)
+        c1 = weighted(3, 2, 0, t1, "last", 10)
         b2 = weighted(3, 1, t1, T, "last", 10)
-        c1 = weighted(3, 2, t0, t1, "last", 10)
-        ab2 = added(a2, b2)
+        nc.sync.dma_start(out[3 * P :, :t1], added(ab1, c1)[:])
         c2 = weighted(3, 2, t1, T, "last", 10)
-        nc.sync.dma_start(out[3 * P :, t0:t1], added(ab1, c1)[:])
+        ab2 = added(a2, b2)
         nc.sync.dma_start(out[3 * P :, t1:], added(ab2, c2)[:])

@@ -23,15 +23,16 @@ ADD = mybir.AluOpType.add
 P = 128
 PAIRS = E // 2
 BLOCKS = K // P
-W2_ROW = 4
 GROUPS = ((0, 4), (4, 8), (8, 10))
-FIRST_FILL_BANKS = (1, 0, 2)
-FILL_BANKS = (6, 7, 2)
-W1_LOADS = ((0, 2), (2, 4), (4, 6), (6, 8), (8, 9), (9, 10))
-PRE_BANKS = ((0, 1), (2, 7))
+FILL_BANKS = (1, 0, 2)
+PRE_BANKS = ((0, 1), (2, 7), (0, 1), (2, 7), (0, 1))
+TURN_BANKS = (3, 4, 5, 3)
+LONE_TURN_BANKS = (4, 5)
+GATHERS = ((0, 3), (3, 6), (6, 8), (8, 10))
+W2_ROW = 4
 HALVES = ((0, 3), (3, 5))
 CHUNKS = T // P
-LAST_CUT = 3 * P
+LAST_CUTS = (2 * P, 4 * P)
 
 
 def tile_moe_cpy_mlp_gelu_kernel(
@@ -52,7 +53,7 @@ def tile_moe_cpy_mlp_gelu_kernel(
         w1 = held.tile([P, E, H], U32, name="w1", align_bytes=64)
         w1s = held.tile([P, E, H], U8, name="w1s", align_bytes=64)
         w2s_first = held.tile([P, E, P], U8, name="w2s_first", align_bytes=64)
-        w2s_rest = held.tile([P, E, K - P], U8, name="w2s_rest", align_bytes=64)
+        w2s = [held.tile([P, K - P], U8, name="w2s%d" % i, align_bytes=64) for i in range(3)]
         w2 = [
             [held.tile([P, hi - lo, P], U32, name="w2_%d_%d" % (b, i), align_bytes=64) for i, (lo, hi) in enumerate(GROUPS)]
             for b in range(2)
@@ -61,7 +62,8 @@ def tile_moe_cpy_mlp_gelu_kernel(
             whole = held.tile([P, E, P], U32, name="w2_%d" % b, align_bytes=64)
             w2.append([whole[:, lo:hi, :] for lo, hi in GROUPS] + [whole])
         ys = [held.tile([P, WIDE], F32, name="y%d" % b, align_bytes=64) for b in range(BLOCKS)]
-        gate_rows = held.tile([P, P], F32, name="gate_rows", align_bytes=64)
+        gate_rows = held.tile([P, T], F32, name="gate_rows", align_bytes=64)
+        gate_cols = held.tile([P, CHUNKS, 2], F32, name="gate_cols", align_bytes=64)
         gates = [held.tile([P, T], F32, name="gate%d" % r, align_bytes=64) for r in range(3)]
         ident = held.tile([P, P], F32, name="ident", align_bytes=64)
         hq = [held.tile([P, 2 * C], U32, name="hq%d" % g, align_bytes=64) for g in range(PAIRS)]
@@ -70,12 +72,23 @@ def tile_moe_cpy_mlp_gelu_kernel(
         def load_words(tile, words):
             nc.sync.dma_start(tile.bitcast(I32), words.rearrange("e p n d -> p e (n d)").bitcast(I32))
 
-        def load_scales(queue, plane, row, scales, rows):
-            for r in rows:
-                queue.dma_start(
+        def load_scales(planes, scales, i, quadrants):
+            lo, hi = GROUPS[i]
+            for q in quadrants:
+                nc.sync.dma_start(
+                    planes[i][32 * q : 32 * q + 4 * (hi - lo), :].bitcast(I32),
+                    scales[lo:hi, 0, 4 * q : 4 * q + 4, :].bitcast(I32),
+                )
+
+        def load_scale_rows(plane, row, scales):
+            for r in range(4):
+                nc.sync.dma_start(
                     plane[row + r : P : 32].bitcast(I32),
                     scales[:, 0, r:16:4, :].rearrange("e q n -> q e n").bitcast(I32),
                 )
+
+        def load_w1(lo, hi):
+            load_words(w1[:, lo:hi, :], w1_words[lo:hi, 0])
 
         def load_w2(b):
             load_words(w2[b][3][:], w2_words[:, 0, :, b * P : (b + 1) * P, :])
@@ -84,8 +97,7 @@ def tile_moe_cpy_mlp_gelu_kernel(
             nc.sync.dma_start(ys[b][:, SLOTS : SLOTS + T], xr[b * P : (b + 1) * P, :])
 
         nc.gpsimd.memset(xs[:].bitcast(I32), 0)
-        nc.gpsimd.memset(gate_rows[:], 0.0)
-        nc.gpsimd.dma_start(gate_rows[0 : 2 * CHUNKS], gate[1:3, 0, :].rearrange("r (j p) -> r j p", p=P))
+        nc.vector.memset(gate_rows[:], 0.0)
         for b in range(BLOCKS):
             nc.vector.memset(ys[b][:, SLOTS + T :], 0.0)
 
@@ -97,40 +109,52 @@ def tile_moe_cpy_mlp_gelu_kernel(
         for q in range(4):
             nc.sync.dma_start(xs[32 * q : 32 * q + 4, :].bitcast(I32), x_scales[0, 4 * q : 4 * q + 4, :].bitcast(I32))
         nc.sync.dma_start(slot_list[:], offs)
-        for lo, hi in W1_LOADS:
-            load_words(w1[:, lo:hi, :], w1_words[lo:hi, 0])
-            if lo == 0:
-                load_scales(nc.sync, w1s, 0, w1_scales, range(4))
-        load_scales(nc.sync, w2s_first, W2_ROW, w2_scales[:, :, :, :P], range(4))
+        nc.sync.dma_start(gate_rows[0:2, :], gate[1:3, 0, :])
+        load_w1(0, 2)
+        load_scale_rows(w1s, 0, w1_scales)
+        for lo, hi in ((2, 4), (4, 6), (6, 8), (8, 9), (9, 10)):
+            load_w1(lo, hi)
+        load_scale_rows(w2s_first, W2_ROW, w2_scales[:, :, :, :P])
         for i, (lo, hi) in enumerate(GROUPS):
             load_words(w2[0][i][:], w2_words[lo:hi, 0, :, 0:P, :])
-        nc.sync.dma_start(choice_lists[0][:], pos1)
         load_xr(0)
+        nc.sync.dma_start(choice_lists[0][:], pos1)
         nc.sync.dma_start(gates[0][:], gate[0])
         nc.sync.dma_start(choice_lists[1][:], pos2)
         nc.sync.dma_start(choice_lists[2][:], pos3)
-        load_scales(nc.sync, w2s_rest, W2_ROW, w2_scales[:, :, :, P:], range(4))
         for i, (lo, hi) in enumerate(GROUPS):
             load_words(w2[1][i][:], w2_words[lo:hi, 0, :, P : 2 * P, :])
-        load_xr(1)
+            load_scales(w2s, w2_scales[:, :, :, P:], i, range(4))
+            if i == 1:
+                load_xr(1)
         for b in range(2, BLOCKS):
             load_w2(b)
             load_xr(b)
 
-        xg = [held.tile([P, 2 * C], U32, name="xg%d" % g, align_bytes=64) for g in range(PAIRS)]
-        xgs = [held.tile([P, 2 * C], U8, name="xgs%d" % g, align_bytes=64) for g in range(PAIRS)]
-        for g in range(PAIRS):
-            picks = slot_list[:, g * 2 * C // 16 : (g + 1) * 2 * C // 16]
-            nc.vector.tensor_copy(xg[g][:], xw[:].indirect(picks))
-            nc.vector.tensor_copy(xgs[g][:], xs[:].indirect(picks))
+        xg, xgs = [], []
+        for lo, hi in GATHERS:
+            words = held.tile([P, hi - lo, C], U32, name="xg%d" % lo, align_bytes=64)
+            bytes_ = held.tile([P, hi - lo, C], U8, name="xgs%d" % lo, align_bytes=64)
+            picks = slot_list[:, lo * C // 16 : hi * C // 16]
+            nc.vector.tensor_copy(words[:].rearrange("p e c -> p (e c)"), xw[:].indirect(picks))
+            nc.vector.tensor_copy(bytes_[:].rearrange("p e c -> p (e c)"), xs[:].indirect(picks))
+            xg.extend(words[:, e, :] for e in range(hi - lo))
+            xgs.extend(bytes_[:, e, :] for e in range(hi - lo))
 
-        def spread_gate(gate_cols, r, banks):
+        def gate_columns(banks):
+            for i, (lo, hi) in enumerate(HALVES):
+                flipped = psum.tile([P, 3, P], F32, name="flipped", tag="bank%d" % banks[i])
+                for j in range(lo, hi):
+                    nc.tensor.transpose(flipped[:, j - lo, :], gate_rows[:, j * P : (j + 1) * P], ident[:])
+                nc.scalar.copy(gate_cols[:, lo:hi, :], flipped[:, : hi - lo, 0:2])
+
+        def spread_gate(r, banks):
             for i, (lo, hi) in enumerate(HALVES):
                 spread = psum.tile([P, 3 * P], F32, name="spread", tag="bank%d" % banks[i])
                 for j in range(lo, hi):
                     nc.tensor.transpose(
                         spread[:, (j - lo) * P : (j - lo + 1) * P],
-                        gate_cols[:, (r - 1) * CHUNKS + j : (r - 1) * CHUNKS + j + 1].to_broadcast([P, P]),
+                        gate_cols[:, j, r - 1 : r].to_broadcast([P, P]),
                         ident[:],
                     )
                 nc.scalar.copy(gates[r][:, lo * P : hi * P], spread[:, : (hi - lo) * P])
@@ -140,13 +164,13 @@ def tile_moe_cpy_mlp_gelu_kernel(
         def first_layer(g):
             h_rows[g] = ring.tile([P, 2, 2, P, 2], BF16, name="h_rows", tag="h_rows", bufs=4, align_bytes=64)
             for half in range(2):
-                pre = psum.tile([P, 2, H // 2], F32, name="pre", tag="bank%d" % PRE_BANKS[g % 2][half])
+                pre = psum.tile([P, 2, H // 2], F32, name="pre", tag="bank%d" % PRE_BANKS[g][half])
                 cols = slice(half * H // 2, (half + 1) * H // 2)
                 for a in range(2):
                     nc.tensor.matmul_mx(
                         out=pre[:, a, :],
-                        lhsT=xg[g][:, a * C : (a + 1) * C].bitcast(FP8X4),
-                        lhsT_scale=xgs[g][:, a * C : (a + 1) * C],
+                        lhsT=xg[2 * g + a].bitcast(FP8X4),
+                        lhsT_scale=xgs[2 * g + a],
                         rhs=w1[:, 2 * g + a, cols].bitcast(FP8X4),
                         rhs_scale=w1s[:, 2 * g + a, cols],
                         start=True,
@@ -159,7 +183,7 @@ def tile_moe_cpy_mlp_gelu_kernel(
                 )
 
         def turn_and_quantise(g):
-            turned = psum.tile([P, 2, 2, C], F32, name="turned", tag="bank%d" % (3 + g % 3))
+            turned = psum.tile([P, 2, 2, C], F32, name="turned", tag="bank%d" % TURN_BANKS[g])
             pairs = h_rows[g][:].rearrange("s u a p d -> s (u a p d)").bitcast(F32)
             for a in range(2):
                 for u in range(2):
@@ -176,11 +200,11 @@ def tile_moe_cpy_mlp_gelu_kernel(
         def lone_first_layer(e):
             g, a = divmod(e, 2)
             h_rows[e] = ring.tile([P, 2, P, 2], BF16, name="h_lone", tag="h_lone", bufs=2, align_bytes=64)
-            pre = psum.tile([P, H], F32, name="pre", tag="bank%d" % PRE_BANKS[g % 2][a])
+            pre = psum.tile([P, H], F32, name="pre", tag="bank%d" % PRE_BANKS[g][a])
             nc.tensor.matmul_mx(
                 out=pre[:],
-                lhsT=xg[g][:, a * C : (a + 1) * C].bitcast(FP8X4),
-                lhsT_scale=xgs[g][:, a * C : (a + 1) * C],
+                lhsT=xg[e].bitcast(FP8X4),
+                lhsT_scale=xgs[e],
                 rhs=w1[:, e, :].bitcast(FP8X4),
                 rhs_scale=w1s[:, e, :],
                 start=True,
@@ -190,7 +214,7 @@ def tile_moe_cpy_mlp_gelu_kernel(
 
         def lone_turn_and_quantise(e):
             g, a = divmod(e, 2)
-            turned = psum.tile([P, 2, C], F32, name="turned", tag="bank%d" % (4 + a))
+            turned = psum.tile([P, 2, C], F32, name="turned", tag="bank%d" % LONE_TURN_BANKS[a])
             pairs = h_rows[e][:].rearrange("s u p d -> s (u p d)").bitcast(F32)
             for u in range(2):
                 nc.tensor.transpose(turned[:, u, :], pairs[:, u * P : (u + 1) * P], ident[:])
@@ -203,13 +227,13 @@ def tile_moe_cpy_mlp_gelu_kernel(
 
         def second_layer(b, i):
             lo, hi = GROUPS[i]
-            acc = psum.tile([P, 4 * C], F32, name="acc", tag="bank%d" % (FILL_BANKS if b else FIRST_FILL_BANKS)[i])
+            acc = psum.tile([P, 4 * C], F32, name="acc", tag="bank%d" % FILL_BANKS[i])
             for e in range(lo, hi):
                 cols = slice((e % 2) * C, (e % 2 + 1) * C)
                 nc.tensor.matmul_mx(
                     out=acc[:, (e - lo) * C : (e - lo + 1) * C],
                     lhsT=w2[b][i][:, e - lo, :].bitcast(FP8X4),
-                    lhsT_scale=w2s_rest[W2_ROW:, e, (b - 1) * P : b * P] if b else w2s_first[W2_ROW:, e, :],
+                    lhsT_scale=w2s[i][4 * (e - lo) :, (b - 1) * P : b * P] if b else w2s_first[W2_ROW:, e, :],
                     rhs=hq[e // 2][:, cols].bitcast(FP8X4),
                     rhs_scale=hs[e // 2][:, cols],
                     start=True,
@@ -227,9 +251,9 @@ def tile_moe_cpy_mlp_gelu_kernel(
             )
             return term
 
-        def summed_on_tensor(terms, into, i):
+        def summed_on_tensor(terms, into, i, bank):
             n = into.shape[1] // P
-            total = psum.tile([P, 3 * P], F32, name="total", tag="bank%d" % FILL_BANKS[i])
+            total = psum.tile([P, 3 * P], F32, name="total", tag="bank%d" % bank)
             for j in range(n):
                 for r in range(3):
                     nc.tensor.matmul(
@@ -247,17 +271,20 @@ def tile_moe_cpy_mlp_gelu_kernel(
                 nc.tensor.transpose(back[:, j * P : (j + 1) * P], by_token[:, j * P : (j + 1) * P], ident[:])
             nc.scalar.copy(into, back[:, : n * P])
 
-        def combined(b, by_halves):
+        def weighted_terms(b, by_halves):
             result = ring.tile([P, T], F32, name="result", tag="result", bufs=2, align_bytes=64)
             if by_halves:
-                terms = [[weighted(b, r, lo * P, hi * P, "term", 12)[:] for r in range(3)] for lo, hi in HALVES]
-            else:
-                whole = [weighted(b, r, 0, T, "term", 12) for r in range(3)]
-                terms = [[t[:, lo * P : hi * P] for t in whole] for lo, hi in HALVES]
-            for i, (lo, hi) in enumerate(HALVES):
-                summed_on_tensor(terms[i], result[:, lo * P : hi * P], i)
-            nc.scalar.dma_start(out[b * P : (b + 1) * P, :], result[:])
+                return [[weighted(b, r, lo * P, hi * P, "term", 12)[:] for r in range(3)] for lo, hi in HALVES], result
+            whole = [weighted(b, r, 0, T, "term", 12) for r in range(3)]
+            return [[t[:, lo * P : hi * P] for t in whole] for lo, hi in HALVES], result
 
+        def fill(b):
+            for i in range(3):
+                second_layer(b, i)
+
+        gate_columns((3, 4))
+        spread_gate(1, (5, 6))
+        spread_gate(2, (3, 4))
         first_layer(0)
         for g in range(PAIRS - 1):
             if g + 1 < PAIRS - 1:
@@ -266,39 +293,40 @@ def tile_moe_cpy_mlp_gelu_kernel(
                 lone_first_layer(E - 2)
                 lone_first_layer(E - 1)
             turn_and_quantise(g)
-        flipped = psum.tile([P, P], F32, name="flipped", tag="bank7")
-        nc.tensor.transpose(flipped[:], gate_rows[:], ident[:])
         lone_turn_and_quantise(E - 2)
         lone_turn_and_quantise(E - 1)
         second_layer(0, 0)
         second_layer(0, 1)
         second_layer(0, 2)
-        gate_cols = held.tile([P, 2 * CHUNKS], F32, name="gate_cols", tag="w2_0_2", align_bytes=64)
-        nc.scalar.copy(gate_cols[:], flipped[:, 0 : 2 * CHUNKS])
-        spread_gate(gate_cols, 1, (1, 0))
-        spread_gate(gate_cols, 2, (6, 7))
+        fill(1)
+        terms, result = weighted_terms(0, False)
+        summed_on_tensor(terms[0], result[:, : 3 * P], 0, 2)
+        fill(2)
+        summed_on_tensor(terms[1], result[:, 3 * P :], 1, 2)
+        nc.scalar.dma_start(out[:P, :], result[:])
+        fill(3)
         for b in (1, 2):
-            for i in range(3):
-                second_layer(b, i)
-        combined(0, False)
-        combined(1, False)
-        for i in range(3):
-            second_layer(3, i)
-        combined(2, True)
+            terms, result = weighted_terms(b, b == 2)
+            for i, (lo, hi) in enumerate(HALVES):
+                summed_on_tensor(terms[i], result[:, lo * P : hi * P], i, ((2, 1), (0, 2))[b - 1][i])
+            nc.scalar.dma_start(out[b * P : (b + 1) * P, :], result[:])
 
         def added(x, y):
             both = ring.tile(list(x.shape), F32, name="both", tag="last", bufs=10, align_bytes=64)
             nc.vector.tensor_tensor(both[:], x[:], y[:], ADD)
             return both
 
-        t1 = LAST_CUT
-        a1 = weighted(3, 0, 0, t1, "last", 10)
-        b1 = weighted(3, 1, 0, t1, "last", 10)
+        t0, t1 = LAST_CUTS
+        front = ring.tile([P, t0], F32, name="front", tag="result", bufs=2, align_bytes=64)
+        summed_on_tensor([weighted(3, r, 0, t0, "term", 12)[:] for r in range(3)], front[:], 0, 1)
+        nc.scalar.dma_start(out[3 * P :, :t0], front[:])
+        a1 = weighted(3, 0, t0, t1, "last", 10)
+        b1 = weighted(3, 1, t0, t1, "last", 10)
         a2 = weighted(3, 0, t1, T, "last", 10)
         ab1 = added(a1, b1)
-        c1 = weighted(3, 2, 0, t1, "last", 10)
         b2 = weighted(3, 1, t1, T, "last", 10)
-        nc.sync.dma_start(out[3 * P :, :t1], added(ab1, c1)[:])
-        c2 = weighted(3, 2, t1, T, "last", 10)
+        c1 = weighted(3, 2, t0, t1, "last", 10)
         ab2 = added(a2, b2)
+        c2 = weighted(3, 2, t1, T, "last", 10)
+        nc.sync.dma_start(out[3 * P :, t0:t1], added(ab1, c1)[:])
         nc.sync.dma_start(out[3 * P :, t1:], added(ab2, c2)[:])

@@ -66,8 +66,9 @@ def tile_moe_cpy_mlp_gelu_kernel(
         gate_cols = held.tile([P, CHUNKS, 2], F32, name="gate_cols", align_bytes=64)
         gates = [held.tile([P, T], F32, name="gate%d" % r, align_bytes=64) for r in range(3)]
         ident = held.tile([P, P], F32, name="ident", align_bytes=64)
-        hq = [held.tile([P, 2 * C], U32, name="hq%d" % g, align_bytes=64) for g in range(PAIRS)]
-        hs = [held.tile([P, 2 * C], U8, name="hs%d" % g, align_bytes=64) for g in range(PAIRS)]
+        hq = [held.tile([P, (hi - lo) * C], U32, name="hq%d" % lo, align_bytes=64) for lo, hi in GROUPS]
+        hs = [held.tile([P, (hi - lo) * C], U8, name="hs%d" % lo, align_bytes=64) for lo, hi in GROUPS]
+        h_cols = [held.tile([P, (hi - lo) * C * 4], BF16, name="h_cols%d" % lo, align_bytes=64) for lo, hi in GROUPS]
 
         def load_words(tile, words):
             nc.sync.dma_start(tile.bitcast(I32), words.rearrange("e p n d -> p e (n d)").bitcast(I32))
@@ -117,10 +118,10 @@ def tile_moe_cpy_mlp_gelu_kernel(
         load_scale_rows(w2s_first, W2_ROW, w2_scales[:, :, :, :P])
         for i, (lo, hi) in enumerate(GROUPS):
             load_words(w2[0][i][:], w2_words[lo:hi, 0, :, 0:P, :])
+        nc.sync.dma_start(choice_lists[1][:], pos2)
         load_xr(0)
         nc.sync.dma_start(choice_lists[0][:], pos1)
         nc.sync.dma_start(gates[0][:], gate[0])
-        nc.sync.dma_start(choice_lists[1][:], pos2)
         nc.sync.dma_start(choice_lists[2][:], pos3)
         for i, (lo, hi) in enumerate(GROUPS):
             load_words(w2[1][i][:], w2_words[lo:hi, 0, :, P : 2 * P, :])
@@ -188,14 +189,11 @@ def tile_moe_cpy_mlp_gelu_kernel(
             for a in range(2):
                 for u in range(2):
                     nc.tensor.transpose(turned[:, a, u, :], pairs[:, (2 * u + a) * P : (2 * u + a + 1) * P], ident[:])
-            h_cols = ring.tile([P, 2 * C * 4], BF16, name="h_cols", tag="h_cols", bufs=5, align_bytes=64)
-            dst = h_cols[:].bitcast(F32).rearrange("p (a s u) -> p a s u", a=2, u=2)
-            src = turned[:].rearrange("p a u s -> p a s u")
-            if g < 1:
-                nc.scalar.copy(dst, src)
-            else:
-                nc.vector.tensor_copy(dst, src)
-            nc.vector.quantize_mx(out=hq[g][:].bitcast(FP8X4), scales=hs[g][:], in_=h_cols[:])
+            i, a = divmod(g, 2)
+            dst = h_cols[i][:, a * 8 * C : (a + 1) * 8 * C].bitcast(F32).rearrange("p (a s u) -> p a s u", a=2, u=2)
+            nc.vector.tensor_copy(dst, turned[:].rearrange("p a u s -> p a s u"))
+            if a:
+                nc.vector.quantize_mx(out=hq[i][:].bitcast(FP8X4), scales=hs[i][:], in_=h_cols[i][:])
 
         def lone_first_layer(e):
             g, a = divmod(e, 2)
@@ -218,24 +216,22 @@ def tile_moe_cpy_mlp_gelu_kernel(
             pairs = h_rows[e][:].rearrange("s u p d -> s (u p d)").bitcast(F32)
             for u in range(2):
                 nc.tensor.transpose(turned[:, u, :], pairs[:, u * P : (u + 1) * P], ident[:])
-            h_cols = ring.tile([P, C * 4], BF16, name="h_cols_lone", tag="h_cols_lone%d" % a, bufs=1, align_bytes=64)
-            nc.scalar.copy(
-                h_cols[:].bitcast(F32).rearrange("p (s u) -> p s u", u=2), turned[:].rearrange("p u s -> p s u")
-            )
+            part = h_cols[2][:, a * 4 * C : (a + 1) * 4 * C]
+            nc.scalar.copy(part.bitcast(F32).rearrange("p (s u) -> p s u", u=2), turned[:].rearrange("p u s -> p s u"))
             cols = slice(a * C, (a + 1) * C)
-            nc.vector.quantize_mx(out=hq[g][:, cols].bitcast(FP8X4), scales=hs[g][:, cols], in_=h_cols[:])
+            nc.vector.quantize_mx(out=hq[2][:, cols].bitcast(FP8X4), scales=hs[2][:, cols], in_=part)
 
         def second_layer(b, i):
             lo, hi = GROUPS[i]
             acc = psum.tile([P, 4 * C], F32, name="acc", tag="bank%d" % FILL_BANKS[i])
             for e in range(lo, hi):
-                cols = slice((e % 2) * C, (e % 2 + 1) * C)
+                cols = slice((e - lo) * C, (e - lo + 1) * C)
                 nc.tensor.matmul_mx(
-                    out=acc[:, (e - lo) * C : (e - lo + 1) * C],
+                    out=acc[:, cols],
                     lhsT=w2[b][i][:, e - lo, :].bitcast(FP8X4),
                     lhsT_scale=w2s[i][4 * (e - lo) :, (b - 1) * P : b * P] if b else w2s_first[W2_ROW:, e, :],
-                    rhs=hq[e // 2][:, cols].bitcast(FP8X4),
-                    rhs_scale=hs[e // 2][:, cols],
+                    rhs=hq[i][:, cols].bitcast(FP8X4),
+                    rhs_scale=hs[i][:, cols],
                     start=True,
                     stop=True,
                 )
@@ -275,7 +271,7 @@ def tile_moe_cpy_mlp_gelu_kernel(
             result = ring.tile([P, T], F32, name="result", tag="result", bufs=2, align_bytes=64)
             if by_halves:
                 return [[weighted(b, r, lo * P, hi * P, "term", 12)[:] for r in range(3)] for lo, hi in HALVES], result
-            whole = [weighted(b, r, 0, T, "term", 12) for r in range(3)]
+            whole = [weighted(b, r, 0, T, "term", 12) for r in (1, 0, 2)]
             return [[t[:, lo * P : hi * P] for t in whole] for lo, hi in HALVES], result
 
         def fill(b):
@@ -284,7 +280,6 @@ def tile_moe_cpy_mlp_gelu_kernel(
 
         gate_columns((3, 4))
         spread_gate(1, (5, 6))
-        spread_gate(2, (3, 4))
         first_layer(0)
         for g in range(PAIRS - 1):
             if g + 1 < PAIRS - 1:
@@ -298,6 +293,7 @@ def tile_moe_cpy_mlp_gelu_kernel(
         second_layer(0, 0)
         second_layer(0, 1)
         second_layer(0, 2)
+        spread_gate(2, (2, 2))
         fill(1)
         terms, result = weighted_terms(0, False)
         summed_on_tensor(terms[0], result[:, : 3 * P], 0, 2)

@@ -45,6 +45,8 @@ def tile_moe_cpy_mlp_gelu_kernel(
         ring = ctx.enter_context(tc.tile_pool(name="ring", bufs=2))
         psum = ctx.enter_context(tc.psum_pool(name="psum", bufs=1))
 
+        banks = [psum.tile([P, 4 * P], F32, name="bank%d" % i) for i in range(8)]
+
         slot_list = lists.tile([P, SLOTS // 16], U16, name="slot_list")
         choice_lists = [lists.tile([P, T // 16], U16, name="choice_list%d" % r) for r in range(3)]
 
@@ -52,15 +54,8 @@ def tile_moe_cpy_mlp_gelu_kernel(
         xs = held.tile([P, T], U8, name="xs", align_bytes=64)
         w1 = held.tile([P, E, H], U32, name="w1", align_bytes=64)
         w1s = held.tile([P, E, H], U8, name="w1s", align_bytes=64)
-        w2s_first = held.tile([P, E, P], U8, name="w2s_first", align_bytes=64)
-        w2s = [held.tile([P, K - P], U8, name="w2s%d" % i, align_bytes=64) for i in range(3)]
-        w2 = [
-            [held.tile([P, hi - lo, P], U32, name="w2_%d_%d" % (b, i), align_bytes=64) for i, (lo, hi) in enumerate(GROUPS)]
-            for b in range(2)
-        ]
-        for b in range(2, BLOCKS):
-            whole = held.tile([P, E, P], U32, name="w2_%d" % b, align_bytes=64)
-            w2.append([whole[:, lo:hi, :] for lo, hi in GROUPS] + [whole])
+        w2s = [held.tile([P, E, 2 * P], U8, name="w2s%d" % half, align_bytes=64) for half in range(2)]
+        w2 = [held.tile([P, E, 2 * P], U32, name="w2_%d" % half, align_bytes=64) for half in range(2)]
         ys = [held.tile([P, WIDE], F32, name="y%d" % b, align_bytes=64) for b in range(BLOCKS)]
         gate_rows = held.tile([P, T], F32, name="gate_rows", align_bytes=64)
         gate_cols = held.tile([P, CHUNKS, 2], F32, name="gate_cols", align_bytes=64)
@@ -73,14 +68,6 @@ def tile_moe_cpy_mlp_gelu_kernel(
         def load_words(tile, words):
             nc.sync.dma_start(tile.bitcast(I32), words.rearrange("e p n d -> p e (n d)").bitcast(I32))
 
-        def load_scales(planes, scales, i, quadrants):
-            lo, hi = GROUPS[i]
-            for q in quadrants:
-                nc.sync.dma_start(
-                    planes[i][32 * q : 32 * q + 4 * (hi - lo), :].bitcast(I32),
-                    scales[lo:hi, 0, 4 * q : 4 * q + 4, :].bitcast(I32),
-                )
-
         def load_scale_rows(plane, row, scales):
             for r in range(4):
                 nc.sync.dma_start(
@@ -91,8 +78,8 @@ def tile_moe_cpy_mlp_gelu_kernel(
         def load_w1(lo, hi):
             load_words(w1[:, lo:hi, :], w1_words[lo:hi, 0])
 
-        def load_w2(b):
-            load_words(w2[b][3][:], w2_words[:, 0, :, b * P : (b + 1) * P, :])
+        def load_w2(half, lo, hi):
+            load_words(w2[half][:, lo:hi, :], w2_words[lo:hi, 0, :, half * 2 * P : (half + 1) * 2 * P, :])
 
         def load_xr(b):
             nc.sync.dma_start(ys[b][:, SLOTS : SLOTS + T], xr[b * P : (b + 1) * P, :])
@@ -115,22 +102,19 @@ def tile_moe_cpy_mlp_gelu_kernel(
         load_scale_rows(w1s, 0, w1_scales)
         for lo, hi in ((2, 4), (4, 6), (6, 8), (8, 9), (9, 10)):
             load_w1(lo, hi)
-        load_scale_rows(w2s_first, W2_ROW, w2_scales[:, :, :, :P])
-        for i, (lo, hi) in enumerate(GROUPS):
-            load_words(w2[0][i][:], w2_words[lo:hi, 0, :, 0:P, :])
+        load_scale_rows(w2s[0], W2_ROW, w2_scales[:, :, :, : 2 * P])
+        for lo, hi in GROUPS:
+            load_w2(0, lo, hi)
         nc.sync.dma_start(choice_lists[1][:], pos2)
         load_xr(0)
         nc.sync.dma_start(choice_lists[0][:], pos1)
         nc.sync.dma_start(gates[0][:], gate[0])
         nc.sync.dma_start(choice_lists[2][:], pos3)
-        for i, (lo, hi) in enumerate(GROUPS):
-            load_words(w2[1][i][:], w2_words[lo:hi, 0, :, P : 2 * P, :])
-            load_scales(w2s, w2_scales[:, :, :, P:], i, range(4))
-            if i == 1:
-                load_xr(1)
-        for b in range(2, BLOCKS):
-            load_w2(b)
-            load_xr(b)
+        load_xr(1)
+        load_scale_rows(w2s[1], W2_ROW, w2_scales[:, :, :, 2 * P :])
+        load_w2(1, 0, E)
+        load_xr(2)
+        load_xr(3)
 
         xg, xgs = [], []
         for lo, hi in GATHERS:
@@ -142,16 +126,16 @@ def tile_moe_cpy_mlp_gelu_kernel(
             xg.extend(words[:, e, :] for e in range(hi - lo))
             xgs.extend(bytes_[:, e, :] for e in range(hi - lo))
 
-        def gate_columns(banks):
+        def gate_columns(which):
             for i, (lo, hi) in enumerate(HALVES):
-                flipped = psum.tile([P, 3, P], F32, name="flipped", tag="bank%d" % banks[i])
+                flipped = banks[which[i]][:].rearrange("p (j m) -> p j m", m=P)
                 for j in range(lo, hi):
                     nc.tensor.transpose(flipped[:, j - lo, :], gate_rows[:, j * P : (j + 1) * P], ident[:])
                 nc.scalar.copy(gate_cols[:, lo:hi, :], flipped[:, : hi - lo, 0:2])
 
-        def spread_gate(r, banks):
+        def spread_gate(r, which):
             for i, (lo, hi) in enumerate(HALVES):
-                spread = psum.tile([P, 3 * P], F32, name="spread", tag="bank%d" % banks[i])
+                spread = banks[which[i]]
                 for j in range(lo, hi):
                     nc.tensor.transpose(
                         spread[:, (j - lo) * P : (j - lo + 1) * P],
@@ -165,7 +149,7 @@ def tile_moe_cpy_mlp_gelu_kernel(
         def first_layer(g):
             h_rows[g] = ring.tile([P, 2, 2, P, 2], BF16, name="h_rows", tag="h_rows", bufs=4, align_bytes=64)
             for half in range(2):
-                pre = psum.tile([P, 2, H // 2], F32, name="pre", tag="bank%d" % PRE_BANKS[g][half])
+                pre = banks[PRE_BANKS[g][half]][:].rearrange("s (a i) -> s a i", a=2)
                 cols = slice(half * H // 2, (half + 1) * H // 2)
                 for a in range(2):
                     nc.tensor.matmul_mx(
@@ -179,26 +163,26 @@ def tile_moe_cpy_mlp_gelu_kernel(
                     )
                 nc.scalar.activation(
                     h_rows[g][:, :, :, half * P // 2 : (half + 1) * P // 2, :],
-                    pre[:].rearrange("s a (p u d) -> s u a p d", u=2, d=2),
+                    pre.rearrange("s a (p u d) -> s u a p d", u=2, d=2),
                     GELU,
                 )
 
         def turn_and_quantise(g):
-            turned = psum.tile([P, 2, 2, C], F32, name="turned", tag="bank%d" % TURN_BANKS[g])
+            turned = banks[TURN_BANKS[g]][:].rearrange("p (a u s) -> p a u s", a=2, u=2)
             pairs = h_rows[g][:].rearrange("s u a p d -> s (u a p d)").bitcast(F32)
             for a in range(2):
                 for u in range(2):
                     nc.tensor.transpose(turned[:, a, u, :], pairs[:, (2 * u + a) * P : (2 * u + a + 1) * P], ident[:])
             i, a = divmod(g, 2)
             dst = h_cols[i][:, a * 8 * C : (a + 1) * 8 * C].bitcast(F32).rearrange("p (a s u) -> p a s u", a=2, u=2)
-            nc.vector.tensor_copy(dst, turned[:].rearrange("p a u s -> p a s u"))
+            nc.vector.tensor_copy(dst, turned.rearrange("p a u s -> p a s u"))
             if a:
                 nc.vector.quantize_mx(out=hq[i][:].bitcast(FP8X4), scales=hs[i][:], in_=h_cols[i][:])
 
         def lone_first_layer(e):
             g, a = divmod(e, 2)
             h_rows[e] = ring.tile([P, 2, P, 2], BF16, name="h_lone", tag="h_lone", bufs=2, align_bytes=64)
-            pre = psum.tile([P, H], F32, name="pre", tag="bank%d" % PRE_BANKS[g][a])
+            pre = banks[PRE_BANKS[g][a]]
             nc.tensor.matmul_mx(
                 out=pre[:],
                 lhsT=xg[e].bitcast(FP8X4),
@@ -212,24 +196,25 @@ def tile_moe_cpy_mlp_gelu_kernel(
 
         def lone_turn_and_quantise(e):
             g, a = divmod(e, 2)
-            turned = psum.tile([P, 2, C], F32, name="turned", tag="bank%d" % LONE_TURN_BANKS[a])
+            turned = banks[LONE_TURN_BANKS[a]][:, : 2 * C].rearrange("p (u s) -> p u s", u=2)
             pairs = h_rows[e][:].rearrange("s u p d -> s (u p d)").bitcast(F32)
             for u in range(2):
                 nc.tensor.transpose(turned[:, u, :], pairs[:, u * P : (u + 1) * P], ident[:])
             part = h_cols[2][:, a * 4 * C : (a + 1) * 4 * C]
-            nc.scalar.copy(part.bitcast(F32).rearrange("p (s u) -> p s u", u=2), turned[:].rearrange("p u s -> p s u"))
+            nc.scalar.copy(part.bitcast(F32).rearrange("p (s u) -> p s u", u=2), turned.rearrange("p u s -> p s u"))
             cols = slice(a * C, (a + 1) * C)
             nc.vector.quantize_mx(out=hq[2][:, cols].bitcast(FP8X4), scales=hs[2][:, cols], in_=part)
 
-        def second_layer(b, i):
+        def second_layer(b, i, bank):
             lo, hi = GROUPS[i]
-            acc = psum.tile([P, 4 * C], F32, name="acc", tag="bank%d" % FILL_BANKS[i])
+            rows = slice(b % 2 * P, (b % 2 + 1) * P)
+            acc = banks[bank]
             for e in range(lo, hi):
                 cols = slice((e - lo) * C, (e - lo + 1) * C)
                 nc.tensor.matmul_mx(
                     out=acc[:, cols],
-                    lhsT=w2[b][i][:, e - lo, :].bitcast(FP8X4),
-                    lhsT_scale=w2s[i][4 * (e - lo) :, (b - 1) * P : b * P] if b else w2s_first[W2_ROW:, e, :],
+                    lhsT=w2[b // 2][:, e, rows].bitcast(FP8X4),
+                    lhsT_scale=w2s[b // 2][W2_ROW:, e, rows],
                     rhs=hq[i][:, cols].bitcast(FP8X4),
                     rhs_scale=hs[i][:, cols],
                     start=True,
@@ -247,9 +232,9 @@ def tile_moe_cpy_mlp_gelu_kernel(
             )
             return term
 
-        def summed_on_tensor(terms, into, i, bank):
-            n = into.shape[1] // P
-            total = psum.tile([P, 3 * P], F32, name="total", tag="bank%d" % bank)
+        def sum_by_token(terms, bank):
+            n = terms[0].shape[1] // P
+            total = banks[bank]
             for j in range(n):
                 for r in range(3):
                     nc.tensor.matmul(
@@ -260,9 +245,13 @@ def tile_moe_cpy_mlp_gelu_kernel(
                         start=(r == 0),
                         stop=(r == 2),
                     )
-            by_token = ring.tile([P, 3 * P], F32, name="by_token", tag="by_token", bufs=2, align_bytes=64)
+            by_token = ring.tile([P, 3 * P], F32, name="by_token", tag="by_token", bufs=3, align_bytes=64)
             nc.scalar.copy(by_token[:, : n * P], total[:, : n * P])
-            back = psum.tile([P, 3 * P], F32, name="back", tag="bank%d" % (3 + i))
+            return by_token
+
+        def turn_back(by_token, into, bank):
+            n = into.shape[1] // P
+            back = banks[bank]
             for j in range(n):
                 nc.tensor.transpose(back[:, j * P : (j + 1) * P], by_token[:, j * P : (j + 1) * P], ident[:])
             nc.scalar.copy(into, back[:, : n * P])
@@ -274,9 +263,9 @@ def tile_moe_cpy_mlp_gelu_kernel(
             whole = [weighted(b, r, 0, T, "term", 12) for r in (1, 0, 2)]
             return [[t[:, lo * P : hi * P] for t in whole] for lo, hi in HALVES], result
 
-        def fill(b):
+        def fill(b, which):
             for i in range(3):
-                second_layer(b, i)
+                second_layer(b, i, which[i])
 
         gate_columns((3, 4))
         spread_gate(1, (5, 6))
@@ -290,21 +279,22 @@ def tile_moe_cpy_mlp_gelu_kernel(
             turn_and_quantise(g)
         lone_turn_and_quantise(E - 2)
         lone_turn_and_quantise(E - 1)
-        second_layer(0, 0)
-        second_layer(0, 1)
-        second_layer(0, 2)
-        spread_gate(2, (2, 2))
-        fill(1)
+        fill(0, FILL_BANKS)
+        second_layer(1, 2, 1)
+        second_layer(1, 0, 0)
+        spread_gate(2, (2, 1))
+        second_layer(1, 1, 2)
         terms, result = weighted_terms(0, False)
-        summed_on_tensor(terms[0], result[:, : 3 * P], 0, 2)
-        fill(2)
-        summed_on_tensor(terms[1], result[:, 3 * P :], 1, 2)
+        early = sum_by_token(terms[0], 2)
+        fill(2, FILL_BANKS)
+        fill(3, (5, 6, 7))
+        turn_back(early, result[:, : 3 * P], 2)
+        turn_back(sum_by_token(terms[1], 1), result[:, 3 * P :], 4)
         nc.scalar.dma_start(out[:P, :], result[:])
-        fill(3)
         for b in (1, 2):
             terms, result = weighted_terms(b, b == 2)
             for i, (lo, hi) in enumerate(HALVES):
-                summed_on_tensor(terms[i], result[:, lo * P : hi * P], i, ((2, 1), (0, 2))[b - 1][i])
+                turn_back(sum_by_token(terms[i], i), result[:, lo * P : hi * P], 3 + i)
             nc.scalar.dma_start(out[b * P : (b + 1) * P, :], result[:])
 
         def added(x, y):
@@ -314,7 +304,7 @@ def tile_moe_cpy_mlp_gelu_kernel(
 
         t0, t1 = LAST_CUTS
         front = ring.tile([P, t0], F32, name="front", tag="result", bufs=2, align_bytes=64)
-        summed_on_tensor([weighted(3, r, 0, t0, "term", 12)[:] for r in range(3)], front[:], 0, 1)
+        turn_back(sum_by_token([weighted(3, r, 0, t0, "term", 12)[:] for r in range(3)], 0), front[:], 3)
         nc.scalar.dma_start(out[3 * P :, :t0], front[:])
         a1 = weighted(3, 0, t0, t1, "last", 10)
         b1 = weighted(3, 1, t0, t1, "last", 10)

@@ -24,12 +24,12 @@ P = 128
 PAIRS = E // 2
 BLOCKS = K // P
 GROUPS = ((0, 4), (4, 8), (8, 10))
-FILL_BANKS = (1, 0, 2)
-PRE_BANKS = ((0, 1), (2, 7), (0, 1), (2, 7), (0, 1))
-TURN_BANKS = (3, 4, 5, 3)
-LONE_TURN_BANKS = (4, 5)
+FILL_BANKS = (3, 7, 2)
+PRE_BANKS = ((0, 1), (2, 7), (0, 1), (2, 7), (1, 3))
+TURN_BANKS = (4, 0, 5, 1)
+LONE_TURN_BANKS = (6, 4)
 GATHERS = ((0, 3), (3, 6), (6, 8), (8, 10))
-W2_ROW = 4
+PACK = 4
 HALVES = ((0, 3), (3, 5))
 CHUNKS = T // P
 LAST_CUTS = (2 * P, 4 * P)
@@ -53,8 +53,8 @@ def tile_moe_cpy_mlp_gelu_kernel(
         xw = held.tile([P, T], U32, name="xw", align_bytes=64)
         xs = held.tile([P, T], U8, name="xs", align_bytes=64)
         w1 = held.tile([P, E, H], U32, name="w1", align_bytes=64)
-        w1s = held.tile([P, E, H], U8, name="w1s", align_bytes=64)
-        w2s = [held.tile([P, E, 2 * P], U8, name="w2s%d" % half, align_bytes=64) for half in range(2)]
+        w1s = [held.tile([P, H], U8, name="w1s%d" % lo, align_bytes=64) for lo, hi in GROUPS]
+        w2s = [held.tile([P, K], U8, name="w2s%d" % lo, align_bytes=64) for lo, hi in GROUPS]
         w2 = [held.tile([P, E, 2 * P], U32, name="w2_%d" % half, align_bytes=64) for half in range(2)]
         ys = [held.tile([P, WIDE], F32, name="y%d" % b, align_bytes=64) for b in range(BLOCKS)]
         gate_rows = held.tile([P, T], F32, name="gate_rows", align_bytes=64)
@@ -68,11 +68,12 @@ def tile_moe_cpy_mlp_gelu_kernel(
         def load_words(tile, words):
             nc.sync.dma_start(tile.bitcast(I32), words.rearrange("e p n d -> p e (n d)").bitcast(I32))
 
-        def load_scale_rows(plane, row, scales):
-            for r in range(4):
+        def load_scales(planes, scales, i):
+            lo, hi = GROUPS[i]
+            for q in range(4):
                 nc.sync.dma_start(
-                    plane[row + r : P : 32].bitcast(I32),
-                    scales[:, 0, r:16:4, :].rearrange("e q n -> q e n").bitcast(I32),
+                    planes[i][32 * q : 32 * q + 4 * (hi - lo), :].bitcast(I32),
+                    scales[lo:hi, 0, 4 * q : 4 * q + 4, :].bitcast(I32),
                 )
 
         def load_w1(lo, hi):
@@ -99,11 +100,15 @@ def tile_moe_cpy_mlp_gelu_kernel(
         nc.sync.dma_start(slot_list[:], offs)
         nc.sync.dma_start(gate_rows[0:2, :], gate[1:3, 0, :])
         load_w1(0, 2)
-        load_scale_rows(w1s, 0, w1_scales)
-        for lo, hi in ((2, 4), (4, 6), (6, 8), (8, 9), (9, 10)):
-            load_w1(lo, hi)
-        load_scale_rows(w2s[0], W2_ROW, w2_scales[:, :, :, : 2 * P])
-        for lo, hi in GROUPS:
+        load_scales(w1s, w1_scales, 0)
+        load_w1(2, 4)
+        load_scales(w1s, w1_scales, 1)
+        load_w1(4, 8)
+        load_scales(w1s, w1_scales, 2)
+        load_w1(8, 9)
+        load_w1(9, 10)
+        for i, (lo, hi) in enumerate(GROUPS):
+            load_scales(w2s, w2_scales, i)
             load_w2(0, lo, hi)
         nc.sync.dma_start(choice_lists[1][:], pos2)
         load_xr(0)
@@ -111,7 +116,6 @@ def tile_moe_cpy_mlp_gelu_kernel(
         nc.sync.dma_start(gates[0][:], gate[0])
         nc.sync.dma_start(choice_lists[2][:], pos3)
         load_xr(1)
-        load_scale_rows(w2s[1], W2_ROW, w2_scales[:, :, :, 2 * P :])
         load_w2(1, 0, E)
         load_xr(2)
         load_xr(3)
@@ -157,7 +161,7 @@ def tile_moe_cpy_mlp_gelu_kernel(
                         lhsT=xg[2 * g + a].bitcast(FP8X4),
                         lhsT_scale=xgs[2 * g + a],
                         rhs=w1[:, 2 * g + a, cols].bitcast(FP8X4),
-                        rhs_scale=w1s[:, 2 * g + a, cols],
+                        rhs_scale=w1s[g // 2][4 * ((2 * g + a) % PACK) :, cols],
                         start=True,
                         stop=True,
                     )
@@ -188,7 +192,7 @@ def tile_moe_cpy_mlp_gelu_kernel(
                 lhsT=xg[e].bitcast(FP8X4),
                 lhsT_scale=xgs[e],
                 rhs=w1[:, e, :].bitcast(FP8X4),
-                rhs_scale=w1s[:, e, :],
+                rhs_scale=w1s[e // PACK][4 * (e % PACK) :, :],
                 start=True,
                 stop=True,
             )
@@ -214,7 +218,7 @@ def tile_moe_cpy_mlp_gelu_kernel(
                 nc.tensor.matmul_mx(
                     out=acc[:, cols],
                     lhsT=w2[b // 2][:, e, rows].bitcast(FP8X4),
-                    lhsT_scale=w2s[b // 2][W2_ROW:, e, rows],
+                    lhsT_scale=w2s[i][4 * (e - lo) :, b * P : (b + 1) * P],
                     rhs=hq[i][:, cols].bitcast(FP8X4),
                     rhs_scale=hs[i][:, cols],
                     start=True,
@@ -280,21 +284,21 @@ def tile_moe_cpy_mlp_gelu_kernel(
         lone_turn_and_quantise(E - 2)
         lone_turn_and_quantise(E - 1)
         fill(0, FILL_BANKS)
-        second_layer(1, 2, 1)
-        second_layer(1, 0, 0)
-        spread_gate(2, (2, 1))
-        second_layer(1, 1, 2)
+        second_layer(1, 2, 3)
+        spread_gate(2, (2, 3))
+        second_layer(1, 0, 2)
+        second_layer(1, 1, 3)
         terms, result = weighted_terms(0, False)
-        early = sum_by_token(terms[0], 2)
-        fill(2, FILL_BANKS)
+        early = sum_by_token(terms[0], 3)
+        fill(2, (2, 0, 3))
         fill(3, (5, 6, 7))
-        turn_back(early, result[:, : 3 * P], 2)
-        turn_back(sum_by_token(terms[1], 1), result[:, 3 * P :], 4)
+        turn_back(early, result[:, : 3 * P], 3)
+        turn_back(sum_by_token(terms[1], 2), result[:, 3 * P :], 4)
         nc.scalar.dma_start(out[:P, :], result[:])
         for b in (1, 2):
             terms, result = weighted_terms(b, b == 2)
             for i, (lo, hi) in enumerate(HALVES):
-                turn_back(sum_by_token(terms[i], i), result[:, lo * P : hi * P], 3 + i)
+                turn_back(sum_by_token(terms[i], 2 * i), result[:, lo * P : hi * P], 3 + i)
             nc.scalar.dma_start(out[b * P : (b + 1) * P, :], result[:])
 
         def added(x, y):

@@ -24,12 +24,13 @@ P = 128
 PAIRS = E // 2
 BLOCKS = K // P
 GROUPS = ((0, 4), (4, 8), (8, 10))
-FILL_BANKS = (3, 7, 2)
-PRE_BANKS = ((0, 1), (2, 7), (0, 1), (2, 7), (1, 3))
-TURN_BANKS = (4, 0, 5, 1)
-LONE_TURN_BANKS = (6, 4)
+FILL_BANKS = (1, 7, 0)
+PRE_BANKS = ((0, 1), (2, 7), (0, 1), (3, 7), (0, 1))
+TURN_BANKS = (2, 4, 3, 5)
+LONE_TURN_BANKS = (6, 2)
 GATHERS = ((0, 3), (3, 6), (6, 8), (8, 10))
-PACK = 4
+W1_GROUPS = ((0, 2), (2, 6), (6, 10))
+W2_ROW = 4
 HALVES = ((0, 3), (3, 5))
 CHUNKS = T // P
 LAST_CUTS = (2 * P, 4 * P)
@@ -53,8 +54,9 @@ def tile_moe_cpy_mlp_gelu_kernel(
         xw = held.tile([P, T], U32, name="xw", align_bytes=64)
         xs = held.tile([P, T], U8, name="xs", align_bytes=64)
         w1 = held.tile([P, E, H], U32, name="w1", align_bytes=64)
-        w1s = [held.tile([P, H], U8, name="w1s%d" % lo, align_bytes=64) for lo, hi in GROUPS]
-        w2s = [held.tile([P, K], U8, name="w2s%d" % lo, align_bytes=64) for lo, hi in GROUPS]
+        w1s = [held.tile([P, H], U8, name="w1s%d" % lo, align_bytes=64) for lo, hi in W1_GROUPS]
+        w1_plane = [w1s[i][4 * (e - lo) :, :] for i, (lo, hi) in enumerate(W1_GROUPS) for e in range(lo, hi)]
+        w2s = [held.tile([P, E, 2 * P], U8, name="w2s%d" % half, align_bytes=64) for half in range(2)]
         w2 = [held.tile([P, E, 2 * P], U32, name="w2_%d" % half, align_bytes=64) for half in range(2)]
         ys = [held.tile([P, WIDE], F32, name="y%d" % b, align_bytes=64) for b in range(BLOCKS)]
         gate_rows = held.tile([P, T], F32, name="gate_rows", align_bytes=64)
@@ -69,11 +71,18 @@ def tile_moe_cpy_mlp_gelu_kernel(
             nc.sync.dma_start(tile.bitcast(I32), words.rearrange("e p n d -> p e (n d)").bitcast(I32))
 
         def load_scales(planes, scales, i):
-            lo, hi = GROUPS[i]
+            lo, hi = W1_GROUPS[i]
             for q in range(4):
                 nc.sync.dma_start(
                     planes[i][32 * q : 32 * q + 4 * (hi - lo), :].bitcast(I32),
                     scales[lo:hi, 0, 4 * q : 4 * q + 4, :].bitcast(I32),
+                )
+
+        def load_w2_scales(half):
+            for r in range(4):
+                nc.sync.dma_start(
+                    w2s[half][W2_ROW + r : P : 32].bitcast(I32),
+                    w2_scales[:, 0, r:16:4, half * 2 * P : (half + 1) * 2 * P].rearrange("e q n -> q e n").bitcast(I32),
                 )
 
         def load_w1(lo, hi):
@@ -87,11 +96,9 @@ def tile_moe_cpy_mlp_gelu_kernel(
 
         nc.gpsimd.memset(xs[:].bitcast(I32), 0)
         nc.vector.memset(gate_rows[:], 0.0)
-        for b in range(BLOCKS):
+        for b in range(BLOCKS - 1):
             nc.vector.memset(ys[b][:, SLOTS + T :], 0.0)
-
-        warm = held.tile([P, 1], F32, name="warm")
-        nc.scalar.activation(warm[:], ys[0][:, WIDE - 1 :], GELU)
+        nc.scalar.activation(ys[BLOCKS - 1][:, SLOTS + T :], ys[0][:, SLOTS + T :], GELU)
         make_identity(nc, ident[:])
 
         nc.sync.dma_start(xw[:].bitcast(I32), x_words[0].rearrange("p t d -> p (t d)").bitcast(I32))
@@ -102,20 +109,23 @@ def tile_moe_cpy_mlp_gelu_kernel(
         load_w1(0, 2)
         load_scales(w1s, w1_scales, 0)
         load_w1(2, 4)
+        load_w1(4, 6)
         load_scales(w1s, w1_scales, 1)
-        load_w1(4, 8)
+        load_w1(6, 8)
         load_scales(w1s, w1_scales, 2)
         load_w1(8, 9)
         load_w1(9, 10)
-        for i, (lo, hi) in enumerate(GROUPS):
-            load_scales(w2s, w2_scales, i)
+        for lo, hi in GROUPS:
             load_w2(0, lo, hi)
+            if lo == 0:
+                load_w2_scales(0)
         nc.sync.dma_start(choice_lists[1][:], pos2)
         load_xr(0)
         nc.sync.dma_start(choice_lists[0][:], pos1)
         nc.sync.dma_start(gates[0][:], gate[0])
         nc.sync.dma_start(choice_lists[2][:], pos3)
         load_xr(1)
+        load_w2_scales(1)
         load_w2(1, 0, E)
         load_xr(2)
         load_xr(3)
@@ -161,7 +171,7 @@ def tile_moe_cpy_mlp_gelu_kernel(
                         lhsT=xg[2 * g + a].bitcast(FP8X4),
                         lhsT_scale=xgs[2 * g + a],
                         rhs=w1[:, 2 * g + a, cols].bitcast(FP8X4),
-                        rhs_scale=w1s[g // 2][4 * ((2 * g + a) % PACK) :, cols],
+                        rhs_scale=w1_plane[2 * g + a][:, cols],
                         start=True,
                         stop=True,
                     )
@@ -192,7 +202,7 @@ def tile_moe_cpy_mlp_gelu_kernel(
                 lhsT=xg[e].bitcast(FP8X4),
                 lhsT_scale=xgs[e],
                 rhs=w1[:, e, :].bitcast(FP8X4),
-                rhs_scale=w1s[e // PACK][4 * (e % PACK) :, :],
+                rhs_scale=w1_plane[e],
                 start=True,
                 stop=True,
             )
@@ -218,7 +228,7 @@ def tile_moe_cpy_mlp_gelu_kernel(
                 nc.tensor.matmul_mx(
                     out=acc[:, cols],
                     lhsT=w2[b // 2][:, e, rows].bitcast(FP8X4),
-                    lhsT_scale=w2s[i][4 * (e - lo) :, b * P : (b + 1) * P],
+                    lhsT_scale=w2s[b // 2][W2_ROW:, e, rows],
                     rhs=hq[i][:, cols].bitcast(FP8X4),
                     rhs_scale=hs[i][:, cols],
                     start=True,
@@ -284,16 +294,16 @@ def tile_moe_cpy_mlp_gelu_kernel(
         lone_turn_and_quantise(E - 2)
         lone_turn_and_quantise(E - 1)
         fill(0, FILL_BANKS)
-        second_layer(1, 2, 3)
-        spread_gate(2, (2, 3))
-        second_layer(1, 0, 2)
-        second_layer(1, 1, 3)
+        second_layer(1, 2, 1)
+        spread_gate(2, (0, 1))
+        second_layer(1, 0, 0)
+        second_layer(1, 1, 1)
         terms, result = weighted_terms(0, False)
-        early = sum_by_token(terms[0], 3)
-        fill(2, (2, 0, 3))
+        early = sum_by_token(terms[0], 1)
+        fill(2, (0, 2, 1))
         fill(3, (5, 6, 7))
-        turn_back(early, result[:, : 3 * P], 3)
-        turn_back(sum_by_token(terms[1], 2), result[:, 3 * P :], 4)
+        turn_back(early, result[:, : 3 * P], 1)
+        turn_back(sum_by_token(terms[1], 0), result[:, 3 * P :], 4)
         nc.scalar.dma_start(out[:P, :], result[:])
         for b in (1, 2):
             terms, result = weighted_terms(b, b == 2)

@@ -32,6 +32,7 @@ GATHERS = ((0, 3), (3, 6), (6, 8), (8, 10))
 W1_GROUPS = ((0, 2), (2, 6), (6, 10))
 W2_ROW = 4
 HALVES = ((0, 3), (3, 5))
+SHORT_FIRST = ((0, 2), (2, 5))
 CHUNKS = T // P
 LAST_CUTS = (2 * P, 4 * P)
 
@@ -259,7 +260,7 @@ def tile_moe_cpy_mlp_gelu_kernel(
                         start=(r == 0),
                         stop=(r == 2),
                     )
-            by_token = ring.tile([P, 3 * P], F32, name="by_token", tag="by_token", bufs=3, align_bytes=64)
+            by_token = ring.tile([P, 3 * P], F32, name="by_token", tag="by_token", bufs=4, align_bytes=64)
             nc.scalar.copy(by_token[:, : n * P], total[:, : n * P])
             return by_token
 
@@ -271,11 +272,13 @@ def tile_moe_cpy_mlp_gelu_kernel(
             nc.scalar.copy(into, back[:, : n * P])
 
         def weighted_terms(b, by_halves):
-            result = ring.tile([P, T], F32, name="result", tag="result", bufs=2, align_bytes=64)
+            result = ring.tile([P, T], F32, name="result", tag="result", bufs=4, align_bytes=64)
+            cuts = HALVES if by_halves else SHORT_FIRST
+            parts = [result[:, lo * P : hi * P] for lo, hi in cuts] + [result[:]]
             if by_halves:
-                return [[weighted(b, r, lo * P, hi * P, "term", 12)[:] for r in range(3)] for lo, hi in HALVES], result
+                return [[weighted(b, r, lo * P, hi * P, "term", 12)[:] for r in range(3)] for lo, hi in cuts], parts
             whole = [weighted(b, r, 0, T, "term", 12) for r in (1, 0, 2)]
-            return [[t[:, lo * P : hi * P] for t in whole] for lo, hi in HALVES], result
+            return [[t[:, lo * P : hi * P] for t in whole] for lo, hi in cuts], parts
 
         def fill(b, which):
             for i in range(3):
@@ -298,28 +301,37 @@ def tile_moe_cpy_mlp_gelu_kernel(
         spread_gate(2, (0, 1))
         second_layer(1, 0, 0)
         second_layer(1, 1, 1)
-        terms, result = weighted_terms(0, False)
-        early = sum_by_token(terms[0], 1)
-        fill(2, (0, 2, 1))
+        terms0, result0 = weighted_terms(0, False)
+        sum0a = sum_by_token(terms0[0], 1)
+        fill(2, (0, 2, 3))
         fill(3, (5, 6, 7))
-        turn_back(early, result[:, : 3 * P], 1)
-        turn_back(sum_by_token(terms[1], 0), result[:, 3 * P :], 4)
-        nc.scalar.dma_start(out[:P, :], result[:])
-        for b in (1, 2):
-            terms, result = weighted_terms(b, b == 2)
-            for i, (lo, hi) in enumerate(HALVES):
-                turn_back(sum_by_token(terms[i], 2 * i), result[:, lo * P : hi * P], 3 + i)
-            nc.scalar.dma_start(out[b * P : (b + 1) * P, :], result[:])
+        turn_back(sum0a, result0[0], 0)
+        sum0b = sum_by_token(terms0[1], 2)
+        terms1, result1 = weighted_terms(1, False)
+        sum1a = sum_by_token(terms1[0], 3)
+        sum1b = sum_by_token(terms1[1], 5)
+        turn_back(sum0b, result0[1], 4)
+        nc.scalar.dma_start(out[:P, :], result0[2])
+        turn_back(sum1a, result1[0], 1)
+        turn_back(sum1b, result1[1], 0)
+        nc.scalar.dma_start(out[P : 2 * P, :], result1[2])
+        terms2, result2 = weighted_terms(2, True)
+        sum2a = sum_by_token(terms2[0], 5)
+        sum2b = sum_by_token(terms2[1], 1)
+        turn_back(sum2a, result2[0], 2)
+        t0, t1 = LAST_CUTS
+        sum3 = sum_by_token([weighted(3, r, 0, t0, "term", 12)[:] for r in range(3)], 5)
+        turn_back(sum2b, result2[1], 3)
+        nc.scalar.dma_start(out[2 * P : 3 * P, :], result2[2])
+        front = ring.tile([P, t0], F32, name="front", tag="result", bufs=4, align_bytes=64)
+        turn_back(sum3, front[:], 4)
+        nc.scalar.dma_start(out[3 * P :, :t0], front[:])
 
         def added(x, y):
             both = ring.tile(list(x.shape), F32, name="both", tag="last", bufs=10, align_bytes=64)
             nc.vector.tensor_tensor(both[:], x[:], y[:], ADD)
             return both
 
-        t0, t1 = LAST_CUTS
-        front = ring.tile([P, t0], F32, name="front", tag="result", bufs=2, align_bytes=64)
-        turn_back(sum_by_token([weighted(3, r, 0, t0, "term", 12)[:] for r in range(3)], 0), front[:], 3)
-        nc.scalar.dma_start(out[3 * P :, :t0], front[:])
         a1 = weighted(3, 0, t0, t1, "last", 10)
         b1 = weighted(3, 1, t0, t1, "last", 10)
         a2 = weighted(3, 0, t1, T, "last", 10)

@@ -107,10 +107,9 @@ def tile_moe_cpy_mlp_gelu_kernel(
             nc.sync.dma_start(xs[32 * q : 32 * q + 4, :].bitcast(I32), x_scales[0, 4 * q : 4 * q + 4, :].bitcast(I32))
         nc.sync.dma_start(slot_list[:], offs)
         nc.sync.dma_start(gate_rows[0:2, :], gate[1:3, 0, :])
-        load_w1(0, 2)
+        load_w1(0, 3)
         load_scales(w1s, w1_scales, 0)
-        load_w1(2, 4)
-        load_w1(4, 6)
+        load_w1(3, 6)
         load_scales(w1s, w1_scales, 1)
         load_w1(6, 8)
         load_scales(w1s, w1_scales, 2)

@@ -111,9 +111,8 @@ def tile_moe_cpy_mlp_gelu_kernel(
         load_scales(w1s, w1_scales, 0)
         load_w1(3, 6)
         load_scales(w1s, w1_scales, 1)
-        load_w1(6, 8)
+        load_w1(6, 9)
         load_scales(w1s, w1_scales, 2)
-        load_w1(8, 9)
         load_w1(9, 10)
         for lo, hi in GROUPS:
             load_w2(0, lo, hi)
@@ -189,8 +188,14 @@ def tile_moe_cpy_mlp_gelu_kernel(
                     nc.tensor.transpose(turned[:, a, u, :], pairs[:, (2 * u + a) * P : (2 * u + a + 1) * P], ident[:])
             i, a = divmod(g, 2)
             dst = h_cols[i][:, a * 8 * C : (a + 1) * 8 * C].bitcast(F32).rearrange("p (a s u) -> p a s u", a=2, u=2)
-            nc.vector.tensor_copy(dst, turned.rearrange("p a u s -> p a s u"))
-            if a:
+            copy = nc.scalar.copy if g == PAIRS - 2 else nc.vector.tensor_copy
+            copy(dst, turned.rearrange("p a u s -> p a s u"))
+            if i:
+                cols = slice(a * 2 * C, (a + 1) * 2 * C)
+                nc.vector.quantize_mx(
+                    out=hq[i][:, cols].bitcast(FP8X4), scales=hs[i][:, cols], in_=h_cols[i][:, a * 8 * C : (a + 1) * 8 * C]
+                )
+            elif a:
                 nc.vector.quantize_mx(out=hq[i][:].bitcast(FP8X4), scales=hs[i][:], in_=h_cols[i][:])
 
         def lone_first_layer(e):

@@ -17,6 +17,7 @@ U16 = mybir.dt.uint16
 U8 = mybir.dt.uint8
 FP8X4 = mybir.dt.float8_e4m3fn_x4
 GELU = mybir.ActivationFunctionType.Gelu_apprx_tanh
+COPY = mybir.ActivationFunctionType.Copy
 MULT = mybir.AluOpType.mult
 ADD = mybir.AluOpType.add
 
@@ -32,9 +33,10 @@ GATHERS = ((0, 3), (3, 6), (6, 8), (8, 10))
 W1_GROUPS = ((0, 2), (2, 6), (6, 10))
 W2_ROW = 4
 HALVES = ((0, 3), (3, 5))
-SHORT_FIRST = ((0, 2), (2, 5))
 CHUNKS = T // P
 LAST_CUTS = (2 * P, 4 * P)
+SUM_BANKS = ((5, 6), (7, 2), (3, 0))
+BACK_BANKS = ((3, 4), (0, 1), (5, 6))
 
 
 def tile_moe_cpy_mlp_gelu_kernel(
@@ -61,7 +63,7 @@ def tile_moe_cpy_mlp_gelu_kernel(
         w2 = [held.tile([P, E, 2 * P], U32, name="w2_%d" % half, align_bytes=64) for half in range(2)]
         ys = [held.tile([P, WIDE], F32, name="y%d" % b, align_bytes=64) for b in range(BLOCKS)]
         gate_rows = held.tile([P, T], F32, name="gate_rows", align_bytes=64)
-        gate_cols = held.tile([P, CHUNKS, 2], F32, name="gate_cols", align_bytes=64)
+        gate_cols = held.tile([P, CHUNKS, 1], F32, name="gate_cols", align_bytes=64)
         gates = [held.tile([P, T], F32, name="gate%d" % r, align_bytes=64) for r in range(3)]
         ident = held.tile([P, P], F32, name="ident", align_bytes=64)
         hq = [held.tile([P, (hi - lo) * C], U32, name="hq%d" % lo, align_bytes=64) for lo, hi in GROUPS]
@@ -106,7 +108,7 @@ def tile_moe_cpy_mlp_gelu_kernel(
         for q in range(4):
             nc.sync.dma_start(xs[32 * q : 32 * q + 4, :].bitcast(I32), x_scales[0, 4 * q : 4 * q + 4, :].bitcast(I32))
         nc.sync.dma_start(slot_list[:], offs)
-        nc.sync.dma_start(gate_rows[0:2, :], gate[1:3, 0, :])
+        nc.sync.dma_start(gate_rows[0:1, :], gate[1:2, 0, :])
         load_w1(0, 3)
         load_scales(w1s, w1_scales, 0)
         load_w1(3, 6)
@@ -120,9 +122,10 @@ def tile_moe_cpy_mlp_gelu_kernel(
                 load_w2_scales(0)
         nc.sync.dma_start(choice_lists[1][:], pos2)
         load_xr(0)
+        nc.sync.dma_start(choice_lists[2][:], pos3)
         nc.sync.dma_start(choice_lists[0][:], pos1)
         nc.sync.dma_start(gates[0][:], gate[0])
-        nc.sync.dma_start(choice_lists[2][:], pos3)
+        nc.sync.dma_start(gates[2][:], gate[2])
         load_xr(1)
         load_w2_scales(1)
         load_w2(1, 0, E)
@@ -144,7 +147,7 @@ def tile_moe_cpy_mlp_gelu_kernel(
                 flipped = banks[which[i]][:].rearrange("p (j m) -> p j m", m=P)
                 for j in range(lo, hi):
                     nc.tensor.transpose(flipped[:, j - lo, :], gate_rows[:, j * P : (j + 1) * P], ident[:])
-                nc.scalar.copy(gate_cols[:, lo:hi, :], flipped[:, : hi - lo, 0:2])
+                nc.scalar.copy(gate_cols[:, lo:hi, :], flipped[:, : hi - lo, 0:1])
 
         def spread_gate(r, which):
             for i, (lo, hi) in enumerate(HALVES):
@@ -264,7 +267,7 @@ def tile_moe_cpy_mlp_gelu_kernel(
                         start=(r == 0),
                         stop=(r == 2),
                     )
-            by_token = ring.tile([P, 3 * P], F32, name="by_token", tag="by_token", bufs=4, align_bytes=64)
+            by_token = ring.tile([P, 3 * P], F32, name="by_token", tag="by_token", bufs=7, align_bytes=64)
             nc.scalar.copy(by_token[:, : n * P], total[:, : n * P])
             return by_token
 
@@ -275,18 +278,38 @@ def tile_moe_cpy_mlp_gelu_kernel(
                 nc.tensor.transpose(back[:, j * P : (j + 1) * P], by_token[:, j * P : (j + 1) * P], ident[:])
             nc.scalar.copy(into, back[:, : n * P])
 
-        def weighted_terms(b, by_halves):
-            result = ring.tile([P, T], F32, name="result", tag="result", bufs=4, align_bytes=64)
-            cuts = HALVES if by_halves else SHORT_FIRST
-            parts = [result[:, lo * P : hi * P] for lo, hi in cuts] + [result[:]]
-            if by_halves:
-                return [[weighted(b, r, lo * P, hi * P, "term", 12)[:] for r in range(3)] for lo, hi in cuts], parts
-            whole = [weighted(b, r, 0, T, "term", 12) for r in (1, 0, 2)]
-            return [[t[:, lo * P : hi * P] for t in whole] for lo, hi in cuts], parts
+        def fetched(b, t0, t1):
+            raw = ring.tile([P, t1 - t0], F32, name="raw", tag="raw", bufs=5, align_bytes=64)
+            nc.scalar.activation(raw[:], ys[b][:].indirect(choice_lists[2][:, t0 // 16 : t1 // 16]), COPY)
+            return raw
 
-        def fill(b, which):
-            for i in range(3):
+        def gated(raw, t0, t1):
+            term = ring.tile([P, t1 - t0], F32, name="term", tag="term", bufs=16, align_bytes=64)
+            nc.vector.tensor_tensor(term[:], raw[:], gates[2][:, t0:t1], MULT)
+            return term
+
+        def terms_of(b, raw, t0, t1):
+            return [weighted(b, 1, t0, t1, "term", 16), weighted(b, 0, t0, t1, "term", 16), gated(raw, t0, t1)]
+
+        def sums(b, terms):
+            return [
+                sum_by_token([t[:, lo * P : hi * P] for t in terms], SUM_BANKS[b][i]) for i, (lo, hi) in enumerate(HALVES)
+            ]
+
+        def finish(b, by_token, queue):
+            result = ring.tile([P, T], F32, name="result", tag="result", bufs=4, align_bytes=64)
+            for i, (lo, hi) in enumerate(HALVES):
+                turn_back(by_token[i], result[:, lo * P : hi * P], BACK_BANKS[b][i])
+            queue.dma_start(out[b * P : (b + 1) * P, :], result[:])
+
+        def fill(b, which, order):
+            for i in order:
                 second_layer(b, i, which[i])
+
+        def added(x, y):
+            both = ring.tile(list(x.shape), F32, name="both", tag="last", bufs=4, align_bytes=64)
+            nc.vector.tensor_tensor(both[:], x, y, ADD)
+            return both
 
         gate_columns((3, 4))
         spread_gate(1, (5, 6))
@@ -300,49 +323,35 @@ def tile_moe_cpy_mlp_gelu_kernel(
             turn_and_quantise(g)
         lone_turn_and_quantise(E - 2)
         lone_turn_and_quantise(E - 1)
-        fill(0, FILL_BANKS)
-        second_layer(1, 2, 1)
-        spread_gate(2, (0, 1))
-        second_layer(1, 0, 0)
-        second_layer(1, 1, 1)
-        terms0, result0 = weighted_terms(0, False)
-        sum0a = sum_by_token(terms0[0], 1)
-        fill(2, (0, 2, 3))
-        fill(3, (5, 6, 7))
-        turn_back(sum0a, result0[0], 0)
-        sum0b = sum_by_token(terms0[1], 2)
-        terms1, result1 = weighted_terms(1, False)
-        sum1a = sum_by_token(terms1[0], 3)
-        sum1b = sum_by_token(terms1[1], 5)
-        turn_back(sum0b, result0[1], 4)
-        nc.scalar.dma_start(out[:P, :], result0[2])
-        turn_back(sum1a, result1[0], 1)
-        turn_back(sum1b, result1[1], 0)
-        nc.scalar.dma_start(out[P : 2 * P, :], result1[2])
-        terms2, result2 = weighted_terms(2, True)
-        sum2a = sum_by_token(terms2[0], 5)
-        sum2b = sum_by_token(terms2[1], 1)
-        turn_back(sum2a, result2[0], 2)
+        fill(0, FILL_BANKS, (0, 1, 2))
+        raw0 = fetched(0, 0, T)
+        fill(1, (0, 7, 1), (2, 0, 1))
+        terms0 = terms_of(0, raw0, 0, T)
+        raw1 = fetched(1, 0, T)
+        terms1 = terms_of(1, raw1, 0, T)
+        fill(2, (2, 3, 4), (0, 1, 2))
+        raw2 = fetched(2, 0, T)
+        terms2 = terms_of(2, raw2, 0, T)
+        fill(3, (5, 6, 7), (0, 1, 2))
         t0, t1 = LAST_CUTS
-        sum3 = sum_by_token([weighted(3, r, 0, t0, "term", 12)[:] for r in range(3)], 5)
-        turn_back(sum2b, result2[1], 3)
-        nc.scalar.dma_start(out[2 * P : 3 * P, :], result2[2])
+        raw_front = fetched(3, 0, t0)
+        raw_rest = fetched(3, t0, T)
+        front_terms = terms_of(3, raw_front, 0, t0)
+        sums0 = sums(0, terms0)
+        sums1 = sums(1, terms1)
+        finish(0, sums0, nc.scalar)
+        finish(1, sums1, nc.scalar)
+        sums2 = sums(2, terms2)
+        front_sum = sum_by_token([t[:] for t in front_terms], 1)
+        finish(2, sums2, nc.scalar)
         front = ring.tile([P, t0], F32, name="front", tag="result", bufs=4, align_bytes=64)
-        turn_back(sum3, front[:], 4)
+        turn_back(front_sum, front[:], 7)
         nc.scalar.dma_start(out[3 * P :, :t0], front[:])
 
-        def added(x, y):
-            both = ring.tile(list(x.shape), F32, name="both", tag="last", bufs=10, align_bytes=64)
-            nc.vector.tensor_tensor(both[:], x[:], y[:], ADD)
-            return both
-
-        a1 = weighted(3, 0, t0, t1, "last", 10)
-        b1 = weighted(3, 1, t0, t1, "last", 10)
-        a2 = weighted(3, 0, t1, T, "last", 10)
-        ab1 = added(a1, b1)
-        b2 = weighted(3, 1, t1, T, "last", 10)
-        c1 = weighted(3, 2, t0, t1, "last", 10)
-        ab2 = added(a2, b2)
-        c2 = weighted(3, 2, t1, T, "last", 10)
-        nc.sync.dma_start(out[3 * P :, t0:t1], added(ab1, c1)[:])
-        nc.sync.dma_start(out[3 * P :, t1:], added(ab2, c2)[:])
+        first = weighted(3, 1, t0, T, "term", 16)
+        third = gated(raw_rest, t0, T)
+        second_a = weighted(3, 0, t0, t1, "term", 16)
+        two = added(first[:], third[:])
+        second_b = weighted(3, 0, t1, T, "term", 16)
+        nc.sync.dma_start(out[3 * P :, t0:t1], added(two[:, : t1 - t0], second_a[:])[:])
+        nc.sync.dma_start(out[3 * P :, t1:], added(two[:, t1 - t0 :], second_b[:])[:])

@@ -25,7 +25,6 @@ P = 128
 PAIRS = E // 2
 BLOCKS = K // P
 GROUPS = ((0, 4), (4, 8), (8, 10))
-FILL_BANKS = (1, 7, 0)
 PRE_BANKS = ((0, 1), (2, 7), (0, 1), (3, 7), (0, 1))
 TURN_BANKS = (2, 4, 3, 5)
 LONE_TURN_BANKS = (6, 2)
@@ -34,9 +33,11 @@ W1_GROUPS = ((0, 2), (2, 6), (6, 10))
 W2_ROW = 4
 HALVES = ((0, 3), (3, 5))
 CHUNKS = T // P
-LAST_CUTS = (2 * P, 4 * P)
-SUM_BANKS = ((5, 6), (7, 2), (3, 0))
-BACK_BANKS = ((3, 4), (0, 1), (5, 6))
+FRONT = 3 * P
+Y_BANKS = ((1, 7, 0), (0, 7, 1), (2, 3, 4), (5, 6, 7))
+SUM_BANKS = ((7, 2), (3, 5), (6, 5))
+BACK_BANKS = ((4, 2), (7, 4), (3, 2))
+GATE_BANKS = (1, 0)
 
 
 def tile_moe_cpy_mlp_gelu_kernel(
@@ -63,8 +64,10 @@ def tile_moe_cpy_mlp_gelu_kernel(
         w2 = [held.tile([P, E, 2 * P], U32, name="w2_%d" % half, align_bytes=64) for half in range(2)]
         ys = [held.tile([P, WIDE], F32, name="y%d" % b, align_bytes=64) for b in range(BLOCKS)]
         gate_rows = held.tile([P, T], F32, name="gate_rows", align_bytes=64)
-        gate_cols = held.tile([P, CHUNKS, 1], F32, name="gate_cols", align_bytes=64)
-        gates = [held.tile([P, T], F32, name="gate%d" % r, align_bytes=64) for r in range(3)]
+        gate_cols = held.tile([P, CHUNKS, 2], F32, name="gate_cols", align_bytes=64)
+        gate_first = held.tile([P, T], F32, name="gate_first", align_bytes=64)
+        gate_second = held.tile([P, T], F32, name="gate_second", align_bytes=64)
+        gate_third = [banks[GATE_BANKS[i]][:, : (hi - lo) * P] for i, (lo, hi) in enumerate(HALVES)]
         ident = held.tile([P, P], F32, name="ident", align_bytes=64)
         hq = [held.tile([P, (hi - lo) * C], U32, name="hq%d" % lo, align_bytes=64) for lo, hi in GROUPS]
         hs = [held.tile([P, (hi - lo) * C], U8, name="hs%d" % lo, align_bytes=64) for lo, hi in GROUPS]
@@ -108,7 +111,7 @@ def tile_moe_cpy_mlp_gelu_kernel(
         for q in range(4):
             nc.sync.dma_start(xs[32 * q : 32 * q + 4, :].bitcast(I32), x_scales[0, 4 * q : 4 * q + 4, :].bitcast(I32))
         nc.sync.dma_start(slot_list[:], offs)
-        nc.sync.dma_start(gate_rows[0:1, :], gate[1:2, 0, :])
+        nc.sync.dma_start(gate_rows[0:2, :], gate[1:3, 0, :])
         load_w1(0, 3)
         load_scales(w1s, w1_scales, 0)
         load_w1(3, 6)
@@ -124,8 +127,7 @@ def tile_moe_cpy_mlp_gelu_kernel(
         load_xr(0)
         nc.sync.dma_start(choice_lists[2][:], pos3)
         nc.sync.dma_start(choice_lists[0][:], pos1)
-        nc.sync.dma_start(gates[0][:], gate[0])
-        nc.sync.dma_start(gates[2][:], gate[2])
+        nc.sync.dma_start(gate_first[:], gate[0])
         load_xr(1)
         load_w2_scales(1)
         load_w2(1, 0, E)
@@ -147,18 +149,20 @@ def tile_moe_cpy_mlp_gelu_kernel(
                 flipped = banks[which[i]][:].rearrange("p (j m) -> p j m", m=P)
                 for j in range(lo, hi):
                     nc.tensor.transpose(flipped[:, j - lo, :], gate_rows[:, j * P : (j + 1) * P], ident[:])
-                nc.scalar.copy(gate_cols[:, lo:hi, :], flipped[:, : hi - lo, 0:1])
+                nc.scalar.copy(gate_cols[:, lo:hi, :], flipped[:, : hi - lo, 0:2])
 
-        def spread_gate(r, which):
+        def spread_gate(r, i, into):
+            lo, hi = HALVES[i]
+            for j in range(lo, hi):
+                nc.tensor.transpose(
+                    into[:, (j - lo) * P : (j - lo + 1) * P], gate_cols[:, j, r - 1 : r].to_broadcast([P, P]), ident[:]
+                )
+
+        def spread_second_gate(which):
             for i, (lo, hi) in enumerate(HALVES):
-                spread = banks[which[i]]
-                for j in range(lo, hi):
-                    nc.tensor.transpose(
-                        spread[:, (j - lo) * P : (j - lo + 1) * P],
-                        gate_cols[:, j, r - 1 : r].to_broadcast([P, P]),
-                        ident[:],
-                    )
-                nc.scalar.copy(gates[r][:, lo * P : hi * P], spread[:, : (hi - lo) * P])
+                spread = banks[which[i]][:, : (hi - lo) * P]
+                spread_gate(1, i, spread)
+                nc.scalar.copy(gate_second[:, lo * P : hi * P], spread)
 
         h_rows = {}
 
@@ -230,11 +234,10 @@ def tile_moe_cpy_mlp_gelu_kernel(
         def second_layer(b, i, bank):
             lo, hi = GROUPS[i]
             rows = slice(b % 2 * P, (b % 2 + 1) * P)
-            acc = banks[bank]
             for e in range(lo, hi):
                 cols = slice((e - lo) * C, (e - lo + 1) * C)
                 nc.tensor.matmul_mx(
-                    out=acc[:, cols],
+                    out=banks[bank][:, cols],
                     lhsT=w2[b // 2][:, e, rows].bitcast(FP8X4),
                     lhsT_scale=w2s[b // 2][W2_ROW:, e, rows],
                     rhs=hq[i][:, cols].bitcast(FP8X4),
@@ -242,33 +245,32 @@ def tile_moe_cpy_mlp_gelu_kernel(
                     start=True,
                     stop=True,
                 )
-            if (b, i) == (0, 1):
-                nc.vector.tensor_copy(ys[b][:, lo * C : hi * C], acc[:, : (hi - lo) * C])
-            else:
-                nc.scalar.copy(ys[b][:, lo * C : hi * C], acc[:, : (hi - lo) * C])
 
-        def weighted(b, r, t0, t1, tag, bufs):
-            term = ring.tile([P, t1 - t0], F32, name="term", tag=tag, bufs=bufs, align_bytes=64)
+        def leave_bank(b, i, bank):
+            lo, hi = GROUPS[i]
+            copy = nc.vector.tensor_copy if (b, i) == (0, 1) else nc.scalar.copy
+            copy(ys[b][:, lo * C : hi * C], banks[bank][:, : (hi - lo) * C])
+
+        def weighted(b, r, t0, t1):
+            term = ring.tile([P, t1 - t0], F32, name="term", tag="term", bufs=18, align_bytes=64)
             nc.vector.tensor_tensor(
-                term[:], ys[b][:].indirect(choice_lists[r][:, t0 // 16 : t1 // 16]), gates[r][:, t0:t1], MULT
+                term[:], ys[b][:].indirect(choice_lists[r][:, t0 // 16 : t1 // 16]), (gate_first, gate_second)[r][:, t0:t1], MULT
             )
             return term
 
         def sum_by_token(terms, bank):
-            n = terms[0].shape[1] // P
-            total = banks[bank]
-            for j in range(n):
+            for j in range(terms[0].shape[1] // P):
                 for r in range(3):
                     nc.tensor.matmul(
-                        total[:, j * P : (j + 1) * P],
+                        banks[bank][:, j * P : (j + 1) * P],
                         lhsT=terms[r][:, j * P : (j + 1) * P],
                         rhs=ident[:],
                         is_transpose=True,
                         start=(r == 0),
                         stop=(r == 2),
                     )
-            by_token = ring.tile([P, 3 * P], F32, name="by_token", tag="by_token", bufs=7, align_bytes=64)
-            nc.scalar.copy(by_token[:, : n * P], total[:, : n * P])
+            by_token = ring.tile(list(terms[0].shape), F32, name="by_token", tag="by_token", bufs=6, align_bytes=64)
+            nc.scalar.copy(by_token[:], banks[bank][:, : terms[0].shape[1]])
             return by_token
 
         def turn_back(by_token, into, bank):
@@ -278,41 +280,45 @@ def tile_moe_cpy_mlp_gelu_kernel(
                 nc.tensor.transpose(back[:, j * P : (j + 1) * P], by_token[:, j * P : (j + 1) * P], ident[:])
             nc.scalar.copy(into, back[:, : n * P])
 
-        def fetched(b, t0, t1):
-            raw = ring.tile([P, t1 - t0], F32, name="raw", tag="raw", bufs=5, align_bytes=64)
-            nc.scalar.activation(raw[:], ys[b][:].indirect(choice_lists[2][:, t0 // 16 : t1 // 16]), COPY)
+        def fetched(b, r, t1):
+            raw = ring.tile([P, t1], F32, name="raw", tag="raw", bufs=5, align_bytes=64)
+            nc.scalar.activation(raw[:], ys[b][:].indirect(choice_lists[r][:, : t1 // 16]), COPY)
             return raw
 
-        def gated(raw, t0, t1):
-            term = ring.tile([P, t1 - t0], F32, name="term", tag="term", bufs=16, align_bytes=64)
-            nc.vector.tensor_tensor(term[:], raw[:], gates[2][:, t0:t1], MULT)
+        def gated(raw, gate_part):
+            term = ring.tile(list(raw.shape), F32, name="term", tag="term", bufs=18, align_bytes=64)
+            nc.vector.tensor_tensor(term[:], raw, gate_part, MULT)
             return term
 
-        def terms_of(b, raw, t0, t1):
-            return [weighted(b, 1, t0, t1, "term", 16), weighted(b, 0, t0, t1, "term", 16), gated(raw, t0, t1)]
+        def third_terms(raw):
+            return [gated(raw[:, lo * P : hi * P], gate_third[i])[:] for i, (lo, hi) in enumerate(HALVES)]
 
-        def sums(b, terms):
-            return [
-                sum_by_token([t[:, lo * P : hi * P] for t in terms], SUM_BANKS[b][i]) for i, (lo, hi) in enumerate(HALVES)
-            ]
+        def terms_of(b):
+            raw = fetched(b, 2, T)
+            whole = [weighted(b, r, 0, T) for r in (1, 0)]
+            third = third_terms(raw)
+            return [[t[:, lo * P : hi * P] for t in whole] + [third[i]] for i, (lo, hi) in enumerate(HALVES)]
+
+        def terms_with_front_fetched(b):
+            raw, raw_front = fetched(b, 2, T), fetched(b, 0, FRONT)
+            second, first_rest = weighted(b, 1, 0, T), weighted(b, 0, FRONT, T)
+            third = third_terms(raw)
+            first_front = gated(raw_front[:], gate_first[:, :FRONT])
+            return [[second[:, :FRONT], third[0], first_front[:]], [second[:, FRONT:], third[1], first_rest[:]]]
 
         def finish(b, by_token, queue):
-            result = ring.tile([P, T], F32, name="result", tag="result", bufs=4, align_bytes=64)
             for i, (lo, hi) in enumerate(HALVES):
-                turn_back(by_token[i], result[:, lo * P : hi * P], BACK_BANKS[b][i])
-            queue.dma_start(out[b * P : (b + 1) * P, :], result[:])
-
-        def fill(b, which, order):
-            for i in order:
-                second_layer(b, i, which[i])
+                result = ring.tile([P, (hi - lo) * P], F32, name="result", tag="result", bufs=6, align_bytes=64)
+                turn_back(by_token[i], result[:], BACK_BANKS[b][i])
+                queue.dma_start(out[b * P : (b + 1) * P, lo * P : hi * P], result[:])
 
         def added(x, y):
-            both = ring.tile(list(x.shape), F32, name="both", tag="last", bufs=4, align_bytes=64)
+            both = ring.tile(list(x.shape), F32, name="both", tag="both", bufs=5, align_bytes=64)
             nc.vector.tensor_tensor(both[:], x, y, ADD)
             return both
 
         gate_columns((3, 4))
-        spread_gate(1, (5, 6))
+        spread_second_gate((5, 6))
         first_layer(0)
         for g in range(PAIRS - 1):
             if g + 1 < PAIRS - 1:
@@ -323,35 +329,41 @@ def tile_moe_cpy_mlp_gelu_kernel(
             turn_and_quantise(g)
         lone_turn_and_quantise(E - 2)
         lone_turn_and_quantise(E - 1)
-        fill(0, FILL_BANKS, (0, 1, 2))
-        raw0 = fetched(0, 0, T)
-        fill(1, (0, 7, 1), (2, 0, 1))
-        terms0 = terms_of(0, raw0, 0, T)
-        raw1 = fetched(1, 0, T)
-        terms1 = terms_of(1, raw1, 0, T)
-        fill(2, (2, 3, 4), (0, 1, 2))
-        raw2 = fetched(2, 0, T)
-        terms2 = terms_of(2, raw2, 0, T)
-        fill(3, (5, 6, 7), (0, 1, 2))
-        t0, t1 = LAST_CUTS
-        raw_front = fetched(3, 0, t0)
-        raw_rest = fetched(3, t0, T)
-        front_terms = terms_of(3, raw_front, 0, t0)
-        sums0 = sums(0, terms0)
-        sums1 = sums(1, terms1)
-        finish(0, sums0, nc.scalar)
+        for i in range(3):
+            second_layer(0, i, Y_BANKS[0][i])
+            leave_bank(0, i, Y_BANKS[0][i])
+        for i in (2, 0, 1):
+            second_layer(1, i, Y_BANKS[1][i])
+            leave_bank(1, i, Y_BANKS[1][i])
+        for i in range(2):
+            spread_gate(2, i, gate_third[i])
+        terms0 = terms_of(0)
+        terms1 = terms_with_front_fetched(1)
+        sum0a = sum_by_token(terms0[0], SUM_BANKS[0][0])
+        for b in (2, 3):
+            for i in range(3):
+                second_layer(b, i, Y_BANKS[b][i])
+        for i in range(3):
+            leave_bank(2, i, Y_BANKS[2][i])
+        terms2 = terms_of(2)
+        sum0b = sum_by_token(terms0[1], SUM_BANKS[0][1])
+        for i in range(3):
+            leave_bank(3, i, Y_BANKS[3][i])
+        raw3 = fetched(3, 2, T)
+        finish(0, (sum0a, sum0b), nc.sync)
+        sums1 = [sum_by_token(terms1[i], SUM_BANKS[1][i]) for i in range(2)]
+        sum2a = sum_by_token(terms2[0], SUM_BANKS[2][0])
         finish(1, sums1, nc.scalar)
-        sums2 = sums(2, terms2)
-        front_sum = sum_by_token([t[:] for t in front_terms], 1)
-        finish(2, sums2, nc.scalar)
-        front = ring.tile([P, t0], F32, name="front", tag="result", bufs=4, align_bytes=64)
-        turn_back(front_sum, front[:], 7)
-        nc.scalar.dma_start(out[3 * P :, :t0], front[:])
+        sum2b = sum_by_token(terms2[1], SUM_BANKS[2][1])
+        finish(2, (sum2a, sum2b), nc.scalar)
 
-        first = weighted(3, 1, t0, T, "term", 16)
-        third = gated(raw_rest, t0, T)
-        second_a = weighted(3, 0, t0, t1, "term", 16)
-        two = added(first[:], third[:])
-        second_b = weighted(3, 0, t1, T, "term", 16)
-        nc.sync.dma_start(out[3 * P :, t0:t1], added(two[:, : t1 - t0], second_a[:])[:])
-        nc.sync.dma_start(out[3 * P :, t1:], added(two[:, t1 - t0 :], second_b[:])[:])
+        second = weighted(3, 1, 0, T)
+        first_a = weighted(3, 0, 0, FRONT)
+        third_a = gated(raw3[:, :FRONT], gate_third[0])
+        two_a = added(second[:, :FRONT], first_a[:])
+        first_b = weighted(3, 0, FRONT, T)
+        nc.sync.dma_start(out[3 * P :, :FRONT], added(two_a[:], third_a[:])[:])
+        two_b = added(second[:, FRONT:], first_b[:])
+        third_b = gated(raw3[:, FRONT:], gate_third[1])
+        for lo, hi in ((0, P), (P, 2 * P)):
+            nc.sync.dma_start(out[3 * P :, FRONT + lo : FRONT + hi], added(two_b[:, lo:hi], third_b[:, lo:hi])[:])

@@ -35,8 +35,8 @@ HALVES = ((0, 3), (3, 5))
 CHUNKS = T // P
 FRONT = 3 * P
 Y_BANKS = ((1, 7, 0), (0, 7, 1), (2, 3, 4), (5, 6, 7))
-SUM_BANKS = ((7, 2), (3, 5), (6, 5))
-BACK_BANKS = ((4, 2), (7, 4), (3, 2))
+SUM_BANKS = {1: (2, 3), 2: (3, 4)}
+BACK_BANKS = {1: (4, 2), 2: (5, 6)}
 GATE_BANKS = (1, 0)
 
 
@@ -125,10 +125,10 @@ def tile_moe_cpy_mlp_gelu_kernel(
                 load_w2_scales(0)
         nc.sync.dma_start(choice_lists[1][:], pos2)
         load_xr(0)
+        load_xr(1)
         nc.sync.dma_start(choice_lists[2][:], pos3)
         nc.sync.dma_start(choice_lists[0][:], pos1)
         nc.sync.dma_start(gate_first[:], gate[0])
-        load_xr(1)
         load_w2_scales(1)
         load_w2(1, 0, E)
         load_xr(2)
@@ -252,7 +252,7 @@ def tile_moe_cpy_mlp_gelu_kernel(
             copy(ys[b][:, lo * C : hi * C], banks[bank][:, : (hi - lo) * C])
 
         def weighted(b, r, t0, t1):
-            term = ring.tile([P, t1 - t0], F32, name="term", tag="term", bufs=18, align_bytes=64)
+            term = ring.tile([P, t1 - t0], F32, name="term", tag="term", bufs=20, align_bytes=64)
             nc.vector.tensor_tensor(
                 term[:], ys[b][:].indirect(choice_lists[r][:, t0 // 16 : t1 // 16]), (gate_first, gate_second)[r][:, t0:t1], MULT
             )
@@ -269,7 +269,7 @@ def tile_moe_cpy_mlp_gelu_kernel(
                         start=(r == 0),
                         stop=(r == 2),
                     )
-            by_token = ring.tile(list(terms[0].shape), F32, name="by_token", tag="by_token", bufs=6, align_bytes=64)
+            by_token = ring.tile(list(terms[0].shape), F32, name="by_token", tag="by_token", bufs=4, align_bytes=64)
             nc.scalar.copy(by_token[:], banks[bank][:, : terms[0].shape[1]])
             return by_token
 
@@ -281,39 +281,32 @@ def tile_moe_cpy_mlp_gelu_kernel(
             nc.scalar.copy(into, back[:, : n * P])
 
         def fetched(b, r, t1):
-            raw = ring.tile([P, t1], F32, name="raw", tag="raw", bufs=5, align_bytes=64)
+            raw = ring.tile([P, t1], F32, name="raw", tag="raw", bufs=6, align_bytes=64)
             nc.scalar.activation(raw[:], ys[b][:].indirect(choice_lists[r][:, : t1 // 16]), COPY)
             return raw
 
         def gated(raw, gate_part):
-            term = ring.tile(list(raw.shape), F32, name="term", tag="term", bufs=18, align_bytes=64)
+            term = ring.tile(list(raw.shape), F32, name="term", tag="term", bufs=20, align_bytes=64)
             nc.vector.tensor_tensor(term[:], raw, gate_part, MULT)
             return term
 
         def third_terms(raw):
             return [gated(raw[:, lo * P : hi * P], gate_third[i])[:] for i, (lo, hi) in enumerate(HALVES)]
 
-        def terms_of(b):
+        def terms_of(b, second):
             raw = fetched(b, 2, T)
-            whole = [weighted(b, r, 0, T) for r in (1, 0)]
+            whole = [second, weighted(b, 0, 0, T)]
             third = third_terms(raw)
             return [[t[:, lo * P : hi * P] for t in whole] + [third[i]] for i, (lo, hi) in enumerate(HALVES)]
 
-        def terms_with_front_fetched(b):
-            raw, raw_front = fetched(b, 2, T), fetched(b, 0, FRONT)
-            second, first_rest = weighted(b, 1, 0, T), weighted(b, 0, FRONT, T)
-            third = third_terms(raw)
-            first_front = gated(raw_front[:], gate_first[:, :FRONT])
-            return [[second[:, :FRONT], third[0], first_front[:]], [second[:, FRONT:], third[1], first_rest[:]]]
-
         def finish(b, by_token, queue):
             for i, (lo, hi) in enumerate(HALVES):
-                result = ring.tile([P, (hi - lo) * P], F32, name="result", tag="result", bufs=6, align_bytes=64)
+                result = ring.tile([P, (hi - lo) * P], F32, name="result", tag="result", bufs=4, align_bytes=64)
                 turn_back(by_token[i], result[:], BACK_BANKS[b][i])
                 queue.dma_start(out[b * P : (b + 1) * P, lo * P : hi * P], result[:])
 
         def added(x, y):
-            both = ring.tile(list(x.shape), F32, name="both", tag="both", bufs=5, align_bytes=64)
+            both = ring.tile(list(x.shape), F32, name="both", tag="both", bufs=9, align_bytes=64)
             nc.vector.tensor_tensor(both[:], x, y, ADD)
             return both
 
@@ -337,33 +330,35 @@ def tile_moe_cpy_mlp_gelu_kernel(
             leave_bank(1, i, Y_BANKS[1][i])
         for i in range(2):
             spread_gate(2, i, gate_third[i])
-        terms0 = terms_of(0)
-        terms1 = terms_with_front_fetched(1)
-        sum0a = sum_by_token(terms0[0], SUM_BANKS[0][0])
+        seconds = [weighted(b, 1, 0, T) for b in range(2)]
+        third = third_terms(fetched(0, 2, T))
+        two = [added(seconds[0][:, lo * P : hi * P], third[i]) for i, (lo, hi) in enumerate(HALVES)]
+        first = gated(fetched(0, 0, T)[:], gate_first[:])
+        terms1 = terms_of(1, seconds[1])
+        for i, (lo, hi) in enumerate(HALVES):
+            nc.sync.dma_start(out[:P, lo * P : hi * P], added(two[i][:], first[:, lo * P : hi * P])[:])
         for b in (2, 3):
             for i in range(3):
                 second_layer(b, i, Y_BANKS[b][i])
         for i in range(3):
             leave_bank(2, i, Y_BANKS[2][i])
-        terms2 = terms_of(2)
-        sum0b = sum_by_token(terms0[1], SUM_BANKS[0][1])
+        terms2 = terms_of(2, weighted(2, 1, 0, T))
         for i in range(3):
             leave_bank(3, i, Y_BANKS[3][i])
-        raw3 = fetched(3, 2, T)
-        finish(0, (sum0a, sum0b), nc.sync)
         sums1 = [sum_by_token(terms1[i], SUM_BANKS[1][i]) for i in range(2)]
+        raw3 = fetched(3, 2, T)
+        finish(1, sums1, nc.sync)
         sum2a = sum_by_token(terms2[0], SUM_BANKS[2][0])
-        finish(1, sums1, nc.scalar)
-        sum2b = sum_by_token(terms2[1], SUM_BANKS[2][1])
-        finish(2, (sum2a, sum2b), nc.scalar)
+        raw_front = fetched(3, 0, FRONT)
+        finish(2, (sum2a, sum_by_token(terms2[1], SUM_BANKS[2][1])), nc.scalar)
 
         second = weighted(3, 1, 0, T)
-        first_a = weighted(3, 0, 0, FRONT)
-        third_a = gated(raw3[:, :FRONT], gate_third[0])
-        two_a = added(second[:, :FRONT], first_a[:])
-        first_b = weighted(3, 0, FRONT, T)
-        nc.sync.dma_start(out[3 * P :, :FRONT], added(two_a[:], third_a[:])[:])
-        two_b = added(second[:, FRONT:], first_b[:])
-        third_b = gated(raw3[:, FRONT:], gate_third[1])
-        for lo, hi in ((0, P), (P, 2 * P)):
-            nc.sync.dma_start(out[3 * P :, FRONT + lo : FRONT + hi], added(two_b[:, lo:hi], third_b[:, lo:hi])[:])
+        third = third_terms(raw3)
+        first_rest = weighted(3, 0, FRONT, T)
+        two_rest = added(second[:, FRONT:], third[1])
+        two_front = added(second[:, :FRONT], third[0])
+        nc.sync.dma_start(out[3 * P :, FRONT:], added(two_rest[:], first_rest[:])[:])
+        pieces = (slice(0, 2 * P), slice(2 * P, FRONT))
+        first_front = [gated(raw_front[:, cols], gate_first[:, cols]) for cols in pieces]
+        for i, cols in enumerate(pieces):
+            nc.sync.dma_start(out[3 * P :, cols], added(two_front[:, cols], first_front[i][:])[:])

@@ -34,9 +34,9 @@ W2_ROW = 4
 HALVES = ((0, 3), (3, 5))
 CHUNKS = T // P
 FRONT = 3 * P
-Y_BANKS = ((1, 7, 0), (0, 7, 1), (2, 3, 4), (5, 6, 7))
-SUM_BANKS = {1: (2, 3), 2: (3, 4)}
-BACK_BANKS = {1: (4, 2), 2: (5, 6)}
+Y_BANKS = ((1, 7, 0), (0, 3, 1), (2, 3, 4), (5, 6, 7))
+SUM_BANKS = {1: (2, 3), 2: (5, 6)}
+BACK_BANKS = {1: (4, 2), 2: (7, 3)}
 GATE_BANKS = (1, 0)
 
 
@@ -119,10 +119,9 @@ def tile_moe_cpy_mlp_gelu_kernel(
         load_w1(6, 9)
         load_scales(w1s, w1_scales, 2)
         load_w1(9, 10)
-        for lo, hi in GROUPS:
-            load_w2(0, lo, hi)
-            if lo == 0:
-                load_w2_scales(0)
+        load_w2(0, 0, 4)
+        load_w2_scales(0)
+        load_w2(0, 4, E)
         nc.sync.dma_start(choice_lists[1][:], pos2)
         load_xr(0)
         load_xr(1)
@@ -252,7 +251,7 @@ def tile_moe_cpy_mlp_gelu_kernel(
             copy(ys[b][:, lo * C : hi * C], banks[bank][:, : (hi - lo) * C])
 
         def weighted(b, r, t0, t1):
-            term = ring.tile([P, t1 - t0], F32, name="term", tag="term", bufs=20, align_bytes=64)
+            term = ring.tile([P, t1 - t0], F32, name="term", tag="term", bufs=22, align_bytes=64)
             nc.vector.tensor_tensor(
                 term[:], ys[b][:].indirect(choice_lists[r][:, t0 // 16 : t1 // 16]), (gate_first, gate_second)[r][:, t0:t1], MULT
             )
@@ -286,18 +285,18 @@ def tile_moe_cpy_mlp_gelu_kernel(
             return raw
 
         def gated(raw, gate_part):
-            term = ring.tile(list(raw.shape), F32, name="term", tag="term", bufs=20, align_bytes=64)
+            term = ring.tile(list(raw.shape), F32, name="term", tag="term", bufs=22, align_bytes=64)
             nc.vector.tensor_tensor(term[:], raw, gate_part, MULT)
             return term
 
         def third_terms(raw):
             return [gated(raw[:, lo * P : hi * P], gate_third[i])[:] for i, (lo, hi) in enumerate(HALVES)]
 
-        def terms_of(b, second):
-            raw = fetched(b, 2, T)
-            whole = [second, weighted(b, 0, 0, T)]
-            third = third_terms(raw)
-            return [[t[:, lo * P : hi * P] for t in whole] + [third[i]] for i, (lo, hi) in enumerate(HALVES)]
+        def first_terms(b):
+            return [weighted(b, 0, lo * P, hi * P)[:] for lo, hi in HALVES]
+
+        def by_halves(second, *others):
+            return [[second[:, lo * P : hi * P]] + [t[i] for t in others] for i, (lo, hi) in enumerate(HALVES)]
 
         def finish(b, by_token, queue):
             for i, (lo, hi) in enumerate(HALVES):
@@ -325,7 +324,7 @@ def tile_moe_cpy_mlp_gelu_kernel(
         for i in range(3):
             second_layer(0, i, Y_BANKS[0][i])
             leave_bank(0, i, Y_BANKS[0][i])
-        for i in (2, 0, 1):
+        for i in (1, 2, 0):
             second_layer(1, i, Y_BANKS[1][i])
             leave_bank(1, i, Y_BANKS[1][i])
         for i in range(2):
@@ -334,7 +333,8 @@ def tile_moe_cpy_mlp_gelu_kernel(
         third = third_terms(fetched(0, 2, T))
         two = [added(seconds[0][:, lo * P : hi * P], third[i]) for i, (lo, hi) in enumerate(HALVES)]
         first = gated(fetched(0, 0, T)[:], gate_first[:])
-        terms1 = terms_of(1, seconds[1])
+        raw1 = fetched(1, 2, T)
+        terms1 = by_halves(seconds[1], first_terms(1), third_terms(raw1))
         for i, (lo, hi) in enumerate(HALVES):
             nc.sync.dma_start(out[:P, lo * P : hi * P], added(two[i][:], first[:, lo * P : hi * P])[:])
         for b in (2, 3):
@@ -342,15 +342,16 @@ def tile_moe_cpy_mlp_gelu_kernel(
                 second_layer(b, i, Y_BANKS[b][i])
         for i in range(3):
             leave_bank(2, i, Y_BANKS[2][i])
-        terms2 = terms_of(2, weighted(2, 1, 0, T))
+        terms2 = by_halves(weighted(2, 1, 0, T), third_terms(fetched(2, 2, T)), first_terms(2))
+        sums1 = [sum_by_token(terms1[i], SUM_BANKS[1][i]) for i in range(2)]
         for i in range(3):
             leave_bank(3, i, Y_BANKS[3][i])
-        sums1 = [sum_by_token(terms1[i], SUM_BANKS[1][i]) for i in range(2)]
         raw3 = fetched(3, 2, T)
-        finish(1, sums1, nc.sync)
         sum2a = sum_by_token(terms2[0], SUM_BANKS[2][0])
+        finish(1, sums1, nc.sync)
+        sum2b = sum_by_token(terms2[1], SUM_BANKS[2][1])
         raw_front = fetched(3, 0, FRONT)
-        finish(2, (sum2a, sum_by_token(terms2[1], SUM_BANKS[2][1])), nc.scalar)
+        finish(2, (sum2a, sum2b), nc.scalar)
 
         second = weighted(3, 1, 0, T)
         third = third_terms(raw3)

from contextlib import ExitStack

import concourse.mybir as mybir
from concourse.masks import make_identity

K, T, E, C, H = 512, 640, 10, 128, 512
SLOTS = E * C
PAD = 64
WIDE = SLOTS + T + PAD
FLOPS = 2 * SLOTS * (K * H + H * K)

F32 = mybir.dt.float32
BF16 = mybir.dt.bfloat16
I32 = mybir.dt.int32
U32 = mybir.dt.uint32
U16 = mybir.dt.uint16
U8 = mybir.dt.uint8
FP8X4 = mybir.dt.float8_e4m3fn_x4
GELU = mybir.ActivationFunctionType.Gelu_apprx_tanh
COPY = mybir.ActivationFunctionType.Copy
MULT = mybir.AluOpType.mult
ADD = mybir.AluOpType.add

P = 128
PAIRS = E // 2
BLOCKS = K // P
GROUPS = ((0, 4), (4, 8), (8, 10))
PRE_BANKS = ((0, 1), (2, 7), (0, 1), (3, 7), (0, 1))
TURN_BANKS = (2, 4, 3, 5)
LONE_TURN_BANKS = (6, 2)
GATHERS = ((0, 3), (3, 6), (6, 8), (8, 10))
W1_GROUPS = ((0, 2), (2, 6), (6, 10))
W2_ROW = 4
HALVES = ((0, 3), (3, 5))
CHUNKS = T // P
FRONT = 3 * P
Y_BANKS = ((1, 7, 0), (0, 3, 1), (2, 3, 4), (5, 6, 7))
SUM_BANKS = {1: (2, 3), 2: (5, 6)}
BACK_BANKS = {1: (4, 2), 2: (7, 3)}
GATE_BANKS = (1, 0)


def tile_moe_cpy_mlp_gelu_kernel(
    tc, x_words, x_scales, xr, w1_words, w1_scales, w2_words, w2_scales, gate, offs, pos1, pos2, pos3, out
):
    nc = tc.nc
    with ExitStack() as ctx:
        lists = ctx.enter_context(tc.tile_pool(name="lists", bufs=1))
        held = ctx.enter_context(tc.tile_pool(name="held", bufs=1))
        ring = ctx.enter_context(tc.tile_pool(name="ring", bufs=2))
        psum = ctx.enter_context(tc.psum_pool(name="psum", bufs=1))

        banks = [psum.tile([P, 4 * P], F32, name="bank%d" % i) for i in range(8)]

        slot_list = lists.tile([P, SLOTS // 16], U16, name="slot_list")
        choice_lists = [lists.tile([P, T // 16], U16, name="choice_list%d" % r) for r in range(3)]

        xw = held.tile([P, T], U32, name="xw", align_bytes=64)
        xs = held.tile([P, T], U8, name="xs", align_bytes=64)
        w1 = held.tile([P, E, H], U32, name="w1", align_bytes=64)
        w1s = [held.tile([P, H], U8, name="w1s%d" % lo, align_bytes=64) for lo, hi in W1_GROUPS]
        w1_plane = [w1s[i][4 * (e - lo) :, :] for i, (lo, hi) in enumerate(W1_GROUPS) for e in range(lo, hi)]
        w2s = [held.tile([P, E, 2 * P], U8, name="w2s%d" % half, align_bytes=64) for half in range(2)]
        w2 = [held.tile([P, E, 2 * P], U32, name="w2_%d" % half, align_bytes=64) for half in range(2)]
        ys = [held.tile([P, WIDE], F32, name="y%d" % b, align_bytes=64) for b in range(BLOCKS)]
        gate_rows = held.tile([P, T], F32, name="gate_rows", align_bytes=64)
        gate_cols = held.tile([P, CHUNKS, 2], F32, name="gate_cols", align_bytes=64)
        gate_first = held.tile([P, T], F32, name="gate_first", align_bytes=64)
        gate_second = held.tile([P, T], F32, name="gate_second", align_bytes=64)
        gate_third = [banks[GATE_BANKS[i]][:, : (hi - lo) * P] for i, (lo, hi) in enumerate(HALVES)]
        ident = held.tile([P, P], F32, name="ident", align_bytes=64)
        hq = [held.tile([P, (hi - lo) * C], U32, name="hq%d" % lo, align_bytes=64) for lo, hi in GROUPS]
        hs = [held.tile([P, (hi - lo) * C], U8, name="hs%d" % lo, align_bytes=64) for lo, hi in GROUPS]
        h_cols = [held.tile([P, (hi - lo) * C * 4], BF16, name="h_cols%d" % lo, align_bytes=64) for lo, hi in GROUPS]

        def load_words(tile, words):
            nc.sync.dma_start(tile.bitcast(I32), words.rearrange("e p n d -> p e (n d)").bitcast(I32))

        def load_scales(planes, scales, i):
            lo, hi = W1_GROUPS[i]
            for q in range(4):
                nc.sync.dma_start(
                    planes[i][32 * q : 32 * q + 4 * (hi - lo), :].bitcast(I32),
                    scales[lo:hi, 0, 4 * q : 4 * q + 4, :].bitcast(I32),
                )

        def load_w2_scales(half):
            for r in range(4):
                nc.sync.dma_start(
                    w2s[half][W2_ROW + r : P : 32].bitcast(I32),
                    w2_scales[:, 0, r:16:4, half * 2 * P : (half + 1) * 2 * P].rearrange("e q n -> q e n").bitcast(I32),
                )

        def load_w1(lo, hi):
            load_words(w1[:, lo:hi, :], w1_words[lo:hi, 0])

        def load_w2(half, lo, hi):
            load_words(w2[half][:, lo:hi, :], w2_words[lo:hi, 0, :, half * 2 * P : (half + 1) * 2 * P, :])

        def load_xr(b):
            nc.sync.dma_start(ys[b][:, SLOTS : SLOTS + T], xr[b * P : (b + 1) * P, :])

        nc.gpsimd.memset(xs[:].bitcast(I32), 0)
        nc.vector.memset(gate_rows[:], 0.0)
        for b in range(BLOCKS - 1):
            nc.vector.memset(ys[b][:, SLOTS + T :], 0.0)
        nc.scalar.activation(ys[BLOCKS - 1][:, SLOTS + T :], ys[0][:, SLOTS + T :], GELU)
        make_identity(nc, ident[:])

        nc.sync.dma_start(xw[:].bitcast(I32), x_words[0].rearrange("p t d -> p (t d)").bitcast(I32))
        for q in range(4):
            nc.sync.dma_start(xs[32 * q : 32 * q + 4, :].bitcast(I32), x_scales[0, 4 * q : 4 * q + 4, :].bitcast(I32))
        nc.sync.dma_start(slot_list[:], offs)
        nc.sync.dma_start(gate_rows[0:2, :], gate[1:3, 0, :])
        load_w1(0, 3)
        load_scales(w1s, w1_scales, 0)
        load_w1(3, 6)
        load_scales(w1s, w1_scales, 1)
        load_w1(6, 9)
        load_scales(w1s, w1_scales, 2)
        load_w1(9, 10)
        load_w2(0, 0, 4)
        load_w2_scales(0)
        load_w2(0, 4, E)
        nc.sync.dma_start(choice_lists[1][:], pos2)
        load_xr(0)
        load_xr(1)
        nc.sync.dma_start(choice_lists[2][:], pos3)
        nc.sync.dma_start(choice_lists[0][:], pos1)
        nc.sync.dma_start(gate_first[:], gate[0])
        load_w2_scales(1)
        load_w2(1, 0, E)
        load_xr(2)
        load_xr(3)

        xg, xgs = [], []
        for lo, hi in GATHERS:
            words = held.tile([P, hi - lo, C], U32, name="xg%d" % lo, align_bytes=64)
            bytes_ = held.tile([P, hi - lo, C], U8, name="xgs%d" % lo, align_bytes=64)
            picks = slot_list[:, lo * C // 16 : hi * C // 16]
            nc.vector.tensor_copy(words[:].rearrange("p e c -> p (e c)"), xw[:].indirect(picks))
            nc.vector.tensor_copy(bytes_[:].rearrange("p e c -> p (e c)"), xs[:].indirect(picks))
            xg.extend(words[:, e, :] for e in range(hi - lo))
            xgs.extend(bytes_[:, e, :] for e in range(hi - lo))

        def gate_columns(which):
            for i, (lo, hi) in enumerate(HALVES):
                flipped = banks[which[i]][:].rearrange("p (j m) -> p j m", m=P)
                for j in range(lo, hi):
                    nc.tensor.transpose(flipped[:, j - lo, :], gate_rows[:, j * P : (j + 1) * P], ident[:])
                nc.scalar.copy(gate_cols[:, lo:hi, :], flipped[:, : hi - lo, 0:2])

        def spread_gate(r, i, into):
            lo, hi = HALVES[i]
            for j in range(lo, hi):
                nc.tensor.transpose(
                    into[:, (j - lo) * P : (j - lo + 1) * P], gate_cols[:, j, r - 1 : r].to_broadcast([P, P]), ident[:]
                )

        def spread_second_gate(which):
            for i, (lo, hi) in enumerate(HALVES):
                spread = banks[which[i]][:, : (hi - lo) * P]
                spread_gate(1, i, spread)
                nc.scalar.copy(gate_second[:, lo * P : hi * P], spread)

        h_rows = {}

        def first_layer(g):
            h_rows[g] = ring.tile([P, 2, 2, P, 2], BF16, name="h_rows", tag="h_rows", bufs=4, align_bytes=64)
            for half in range(2):
                pre = banks[PRE_BANKS[g][half]][:].rearrange("s (a i) -> s a i", a=2)
                cols = slice(half * H // 2, (half + 1) * H // 2)
                for a in range(2):
                    nc.tensor.matmul_mx(
                        out=pre[:, a, :],
                        lhsT=xg[2 * g + a].bitcast(FP8X4),
                        lhsT_scale=xgs[2 * g + a],
                        rhs=w1[:, 2 * g + a, cols].bitcast(FP8X4),
                        rhs_scale=w1_plane[2 * g + a][:, cols],
                        start=True,
                        stop=True,
                    )
                nc.scalar.activation(
                    h_rows[g][:, :, :, half * P // 2 : (half + 1) * P // 2, :],
                    pre.rearrange("s a (p u d) -> s u a p d", u=2, d=2),
                    GELU,
                )

        def turn_and_quantise(g):
            turned = banks[TURN_BANKS[g]][:].rearrange("p (a u s) -> p a u s", a=2, u=2)
            pairs = h_rows[g][:].rearrange("s u a p d -> s (u a p d)").bitcast(F32)
            for a in range(2):
                for u in range(2):
                    nc.tensor.transpose(turned[:, a, u, :], pairs[:, (2 * u + a) * P : (2 * u + a + 1) * P], ident[:])
            i, a = divmod(g, 2)
            dst = h_cols[i][:, a * 8 * C : (a + 1) * 8 * C].bitcast(F32).rearrange("p (a s u) -> p a s u", a=2, u=2)
            copy = nc.scalar.copy if g == PAIRS - 2 else nc.vector.tensor_copy
            copy(dst, turned.rearrange("p a u s -> p a s u"))
            if i:
                cols = slice(a * 2 * C, (a + 1) * 2 * C)
                nc.vector.quantize_mx(
                    out=hq[i][:, cols].bitcast(FP8X4), scales=hs[i][:, cols], in_=h_cols[i][:, a * 8 * C : (a + 1) * 8 * C]
                )
            elif a:
                nc.vector.quantize_mx(out=hq[i][:].bitcast(FP8X4), scales=hs[i][:], in_=h_cols[i][:])

        def lone_first_layer(e):
            g, a = divmod(e, 2)
            h_rows[e] = ring.tile([P, 2, P, 2], BF16, name="h_lone", tag="h_lone", bufs=2, align_bytes=64)
            pre = banks[PRE_BANKS[g][a]]
            nc.tensor.matmul_mx(
                out=pre[:],
                lhsT=xg[e].bitcast(FP8X4),
                lhsT_scale=xgs[e],
                rhs=w1[:, e, :].bitcast(FP8X4),
                rhs_scale=w1_plane[e],
                start=True,
                stop=True,
            )
            nc.scalar.activation(h_rows[e][:], pre[:].rearrange("s (p u d) -> s u p d", u=2, d=2), GELU)

        def lone_turn_and_quantise(e):
            g, a = divmod(e, 2)
            turned = banks[LONE_TURN_BANKS[a]][:, : 2 * C].rearrange("p (u s) -> p u s", u=2)
            pairs = h_rows[e][:].rearrange("s u p d -> s (u p d)").bitcast(F32)
            for u in range(2):
                nc.tensor.transpose(turned[:, u, :], pairs[:, u * P : (u + 1) * P], ident[:])
            part = h_cols[2][:, a * 4 * C : (a + 1) * 4 * C]
            nc.scalar.copy(part.bitcast(F32).rearrange("p (s u) -> p s u", u=2), turned.rearrange("p u s -> p s u"))
            cols = slice(a * C, (a + 1) * C)
            nc.vector.quantize_mx(out=hq[2][:, cols].bitcast(FP8X4), scales=hs[2][:, cols], in_=part)

        def second_layer(b, i, bank):
            lo, hi = GROUPS[i]
            rows = slice(b % 2 * P, (b % 2 + 1) * P)
            for e in range(lo, hi):
                cols = slice((e - lo) * C, (e - lo + 1) * C)
                nc.tensor.matmul_mx(
                    out=banks[bank][:, cols],
                    lhsT=w2[b // 2][:, e, rows].bitcast(FP8X4),
                    lhsT_scale=w2s[b // 2][W2_ROW:, e, rows],
                    rhs=hq[i][:, cols].bitcast(FP8X4),
                    rhs_scale=hs[i][:, cols],
                    start=True,
                    stop=True,
                )

        def leave_bank(b, i, bank):
            lo, hi = GROUPS[i]
            copy = nc.vector.tensor_copy if (b, i) == (0, 1) else nc.scalar.copy
            copy(ys[b][:, lo * C : hi * C], banks[bank][:, : (hi - lo) * C])

        def weighted(b, r, t0, t1):
            term = ring.tile([P, t1 - t0], F32, name="term", tag="term", bufs=22, align_bytes=64)
            nc.vector.tensor_tensor(
                term[:], ys[b][:].indirect(choice_lists[r][:, t0 // 16 : t1 // 16]), (gate_first, gate_second)[r][:, t0:t1], MULT
            )
            return term

        def sum_by_token(terms, bank):
            for j in range(terms[0].shape[1] // P):
                for r in range(3):
                    nc.tensor.matmul(
                        banks[bank][:, j * P : (j + 1) * P],
                        lhsT=terms[r][:, j * P : (j + 1) * P],
                        rhs=ident[:],
                        is_transpose=True,
                        start=(r == 0),
                        stop=(r == 2),
                    )
            by_token = ring.tile(list(terms[0].shape), F32, name="by_token", tag="by_token", bufs=4, align_bytes=64)
            nc.scalar.copy(by_token[:], banks[bank][:, : terms[0].shape[1]])
            return by_token

        def turn_back(by_token, into, bank):
            n = into.shape[1] // P
            back = banks[bank]
            for j in range(n):
                nc.tensor.transpose(back[:, j * P : (j + 1) * P], by_token[:, j * P : (j + 1) * P], ident[:])
            nc.scalar.copy(into, back[:, : n * P])

        def fetched(b, r, t1):
            raw = ring.tile([P, t1], F32, name="raw", tag="raw", bufs=6, align_bytes=64)
            nc.scalar.activation(raw[:], ys[b][:].indirect(choice_lists[r][:, : t1 // 16]), COPY)
            return raw

        def gated(raw, gate_part):
            term = ring.tile(list(raw.shape), F32, name="term", tag="term", bufs=22, align_bytes=64)
            nc.vector.tensor_tensor(term[:], raw, gate_part, MULT)
            return term

        def third_terms(raw):
            return [gated(raw[:, lo * P : hi * P], gate_third[i])[:] for i, (lo, hi) in enumerate(HALVES)]

        def first_terms(b):
            return [weighted(b, 0, lo * P, hi * P)[:] for lo, hi in HALVES]

        def by_halves(second, *others):
            return [[second[:, lo * P : hi * P]] + [t[i] for t in others] for i, (lo, hi) in enumerate(HALVES)]

        def finish(b, by_token, queue):
            for i, (lo, hi) in enumerate(HALVES):
                result = ring.tile([P, (hi - lo) * P], F32, name="result", tag="result", bufs=4, align_bytes=64)
                turn_back(by_token[i], result[:], BACK_BANKS[b][i])
                queue.dma_start(out[b * P : (b + 1) * P, lo * P : hi * P], result[:])

        def added(x, y):
            both = ring.tile(list(x.shape), F32, name="both", tag="both", bufs=9, align_bytes=64)
            nc.vector.tensor_tensor(both[:], x, y, ADD)
            return both

        gate_columns((3, 4))
        spread_second_gate((5, 6))
        first_layer(0)
        for g in range(PAIRS - 1):
            if g + 1 < PAIRS - 1:
                first_layer(g + 1)
            else:
                lone_first_layer(E - 2)
                lone_first_layer(E - 1)
            turn_and_quantise(g)
        lone_turn_and_quantise(E - 2)
        lone_turn_and_quantise(E - 1)
        for i in range(3):
            second_layer(0, i, Y_BANKS[0][i])
            leave_bank(0, i, Y_BANKS[0][i])
        for i in (1, 2, 0):
            second_layer(1, i, Y_BANKS[1][i])
            leave_bank(1, i, Y_BANKS[1][i])
        for i in range(2):
            spread_gate(2, i, gate_third[i])
        seconds = [weighted(b, 1, 0, T) for b in range(2)]
        third = third_terms(fetched(0, 2, T))
        two = [added(seconds[0][:, lo * P : hi * P], third[i]) for i, (lo, hi) in enumerate(HALVES)]
        first = gated(fetched(0, 0, T)[:], gate_first[:])
        raw1 = fetched(1, 2, T)
        terms1 = by_halves(seconds[1], first_terms(1), third_terms(raw1))
        for i, (lo, hi) in enumerate(HALVES):
            nc.sync.dma_start(out[:P, lo * P : hi * P], added(two[i][:], first[:, lo * P : hi * P])[:])
        for b in (2, 3):
            for i in range(3):
                second_layer(b, i, Y_BANKS[b][i])
        for i in range(3):
            leave_bank(2, i, Y_BANKS[2][i])
        terms2 = by_halves(weighted(2, 1, 0, T), third_terms(fetched(2, 2, T)), first_terms(2))
        sums1 = [sum_by_token(terms1[i], SUM_BANKS[1][i]) for i in range(2)]
        for i in range(3):
            leave_bank(3, i, Y_BANKS[3][i])
        raw3 = fetched(3, 2, T)
        sum2a = sum_by_token(terms2[0], SUM_BANKS[2][0])
        finish(1, sums1, nc.sync)
        sum2b = sum_by_token(terms2[1], SUM_BANKS[2][1])
        raw_front = fetched(3, 0, FRONT)
        finish(2, (sum2a, sum2b), nc.scalar)

        second = weighted(3, 1, 0, T)
        third = third_terms(raw3)
        first_rest = weighted(3, 0, FRONT, T)
        two_rest = added(second[:, FRONT:], third[1])
        two_front = added(second[:, :FRONT], third[0])
        nc.sync.dma_start(out[3 * P :, FRONT:], added(two_rest[:], first_rest[:])[:])
        pieces = (slice(0, 2 * P), slice(2 * P, FRONT))
        first_front = [gated(raw_front[:, cols], gate_first[:, cols]) for cols in pieces]
        for i, cols in enumerate(pieces):
            nc.sync.dma_start(out[3 * P :, cols], added(two_front[:, cols], first_front[i][:])[:])
